import numpy as np, ml_dtypes
CORES = [3,7,11,15,131,135,139,143]
N = 8
import mx_ref
BF = ml_dtypes.bfloat16
def entries(a):
    return np.ascontiguousarray(a.T).reshape(-1)
def table(e):
    return np.ascontiguousarray(np.reshape(e, (-1, 16)).T).astype(np.int32)
def cols(t, e):
    v = np.concatenate([t.reshape(128, -1, 4), np.zeros((128, 1, 4), BF)], axis=1)
    return np.ascontiguousarray(v[:, e]).reshape(128, -1)
def f(rng, *shape):
    return mx_ref.flush((rng.standard_normal(shape, dtype=np.float32) * np.exp2(rng.integers(-2, 3, shape[:-1] + (1,)))).astype(BF))
def wide(rng, *shape, cols=0):
    v = rng.standard_normal(shape, dtype=np.float32) * np.exp2(rng.integers(-12, 13, shape)).astype(np.float32)
    if cols: v *= np.repeat(np.exp2(rng.integers(-cols, cols + 1, shape[:-2] + (1, shape[-1] // 4))) * (rng.random(shape[:-2] + (1, shape[-1] // 4)) > 0.0625), 4, axis=-1).astype(np.float32)
    return mx_ref.flush(v.astype(BF))
T, S, CAPP = 512, 256, 48
def lists(rng, most=None, own=False, share=False, edge=False):
    o, c, m = [], [], []
    for r in range(N):
        n = np.zeros(N, int)
        if own: n[r] = CAPP
        if most is not None:
            for q in rng.permutation(N)[:most]: n[q] = CAPP
            n = np.minimum(n, np.maximum(0, S - (np.cumsum(n) - n)))
        while n.sum() < S:
            q = rng.integers(0, N)
            if n[q] < CAPP: n[q] += 1
        slots = np.full(N * CAPP, -1); used = []
        for q in range(N):
            k = q * CAPP + rng.permutation(CAPP)[:n[q]]; used += list(k)
            slots[k] = rng.integers(0, T) if share else rng.choice([0, T - 1], n[q]) if edge else rng.integers(0, T, n[q])
        o.append(table(rng.choice([0, T - 1], S) if edge else rng.integers(0, T, S))); c.append(table(slots)); m.append(table(rng.permutation(used)))
    return {"own": np.stack(o), "want": np.stack(c), "slot": np.stack(m)}
def setup_inputs(rng):
    return {"x": f(rng, N, 128, 4 * T), "w": f(rng, N, 128, 512), **lists(rng)}
def setup_inputs_edge(rng):
    return {**setup_inputs(rng), **lists(rng, edge=True)}
def setup_inputs_full(rng):
    return {**setup_inputs(rng), **lists(rng, most=S // CAPP)}
def setup_inputs_self(rng):
    return {**setup_inputs(rng), **lists(rng, own=True)}
def setup_inputs_share(rng):
    return {**setup_inputs(rng), **lists(rng, share=True)}
def setup_inputs_spread(rng):
    d = setup_inputs(rng); d["x"] = wide(rng, N, 128, 4 * T, cols=8); return d
def check_inputs(d):
    b = []
    for r in range(N):
        o, c, m = entries(d["own"][r]), entries(d["want"][r]), entries(d["slot"][r])
        if o.min() < 0 or o.max() >= T: b.append("own")
        if c.min() < -1 or c.max() >= T: b.append("want")
        if m.min() < 0 or m.max() >= N * CAPP or len(set(m.tolist())) != S or (c[m] < 0).any() or (c >= 0).sum() != S: b.append("slot")
    return b
def decode(q):
    out = np.zeros(q[0].shape, np.float32)
    for b in range(4):
        e = np.zeros((128, 128, 4), np.float32); e[np.arange(128), np.arange(128), b] = 1
        out[:, b::4] = mx_ref.matmul(mx_ref.quantize(e.reshape(128, 512).astype(BF)), q)
    return out
def reference(x, w, own, want, slot):
    M = []
    for r in range(N):
        c = entries(want[r])
        arrived = np.concatenate([decode(mx_ref.quantize(cols(x[q], c[q * CAPP:(q + 1) * CAPP]))) for q in range(N)], axis=1)
        far = arrived.reshape(128, -1, 4)[:, entries(slot[r])].reshape(128, -1)
        M.append(mx_ref.quantize(((cols(x[r], entries(own[r])).astype(np.float32) + far) * np.float32(0.5)).astype(BF)))
    y = np.zeros((N, 128, 3 * S), np.float32)
    for r in range(N):
        for i in range(3): y[r][:, S * i:S * i + S] = mx_ref.matmul(mx_ref.quantize(w[r]), M[(r - 1 + i) % N])
    return {"y": y}

@@ -1,0 +1,313 @@
+from concourse.bass import DstId, RemoteDMATransfer, IndirectOffsetOnAxis
+from concourse.mybir import dt, AluOpType, ActivationFunctionType
+
+N, CAPP, S, XC = 8, 48, 256, 512
+G = 4
+H = S // 2
+
+SCRATCH = {
+    "wl": ("sbuf", [128, 24], "int32"),
+    "ol": ("sbuf", [128, 16], "int32"),
+    "sl": ("sbuf", [128, 16], "int32"),
+    "lf": ("sbuf", [128, 12], "int32"),
+    "ln": ("sbuf", [128, 12], "int32"),
+    "fo": ("sbuf", [128, 12], "uint16"),
+    "no": ("sbuf", [128, 16], "uint16"),
+    "wo": ("sbuf", [128, 8], "uint16"),
+    "oo": ("sbuf", [128, 16], "uint16"),
+    "so": ("sbuf", [128, 16], "uint16"),
+    "xt": ("sbuf", [128, 4 * XC], "bfloat16"),
+    "wt": ("sbuf", [128, 512], "bfloat16"),
+    "wq": ("sbuf", [128, 128], "float8_e4m3fn_x4"),
+    "ws": ("sbuf", [128, 128], "uint8"),
+    "e1": ("sbuf", [128, 520], "bfloat16"),
+    "e2": ("sbuf", [128, 520], "bfloat16"),
+    "eq": ("sbuf", [128, 512], "float8_e4m3fn_x4"),
+    "es": ("sbuf", [128, 512], "uint8"),
+    "hf": ("sbuf", [128, 4 * 192], "bfloat16"),
+    "hn": ("sbuf", [128, 4 * 144], "bfloat16"),
+    "ho": ("sbuf", [128, 512], "bfloat16"),
+    "qf": ("sbuf", [128, 192], "float8_e4m3fn_x4"),
+    "qfs": ("sbuf", [128, 192], "uint8"),
+    "qn": ("sbuf", [128, 144], "float8_e4m3fn_x4"),
+    "qns": ("sbuf", [128, 144], "uint8"),
+    "qo": ("sbuf", [128, 128], "float8_e4m3fn_x4"),
+    "qos": ("sbuf", [128, 128], "uint8"),
+    "cf": ("sbuf", [128, 192], "float8_e4m3fn_x4"),
+    "cfs": ("sbuf", [128, 192], "uint8"),
+    "cn": ("sbuf", [128, 192], "float8_e4m3fn_x4"),
+    "cns": ("sbuf", [128, 192], "uint8"),
+    "dw": ("sbuf", [128, 4 * N * CAPP], "float32"),
+    "xo": ("sbuf", [128, 4 * S], "float32"),
+    "m": ("sbuf", [128, 4 * S], "bfloat16"),
+    "mq": ("sbuf", [128, S], "float8_e4m3fn_x4"),
+    "ms": ("sbuf", [128, S], "uint8"),
+    "iq": ("sbuf", [128, S], "float8_e4m3fn_x4"),
+    "is_": ("sbuf", [128, S], "uint8"),
+    "oq": ("sbuf", [128, S], "float8_e4m3fn_x4"),
+    "os_": ("sbuf", [128, S], "uint8"),
+    "yo": ("sbuf", [128, S], "float32"),
+    "yi": ("sbuf", [128, S], "float32"),
+    "yf": ("sbuf", [128, S], "float32"),
+    "pf": ("psum", [128, 2048], "float32"),
+    "pn": ("psum", [128, 2048], "float32"),
+}
+SEMAPHORES = (["want", "xl", "own", "slot", "wl", "sent", "lf", "ln", "cf", "cn", "mi", "mo", "e1", "e2", "eq", "wq",
+               "hoz", "cvw", "cvo", "cvs", "cvf", "cvn", "gfv", "gfs", "gnv", "gns", "gos", "qf", "qn", "qo", "oc", "q0", "q1",
+               "yo", "yi", "yf0", "yf1", "po", "pi", "pf0", "pf1", "st1", "st2"]
+              + ["df%d" % b for b in range(4)] + ["dn%d" % b for b in range(4)]
+              + ["wf%d" % b for b in range(4)] + ["wn%d" % b for b in range(4)]
+              + ["xo%d" % b for b in range(4)] + ["ga0", "ga1"])
+
+
+def bits(engines):
+    m = 0
+    for e in engines:
+        m |= 1 << e
+    return m
+
+
+def rank_program(g, core, T, topo):
+    r = T.rank_of(core)
+    if r is None:
+        return
+    sem = T.sem
+    v, a, pe, sy = g.vector, g.scalar, g.tensor, g.sync
+    COPY = ActivationFunctionType.Copy
+    cores = T.cores
+
+    host = [q for q in range(N) if topo.host(cores[q]) == topo.host(core)]
+    far = [q for q in range(N) if q not in host]
+    near = [q for q in host if q != r]
+    mates = [q for q in near if topo.mates(core, cores[q])]
+    partner = [q for q in near if q not in mates][0]
+    left, right = (r - 1) % N, (r + 1) % N
+    away = left if right == partner else right
+    off_eng = topo.engines(core, cores[far[0]])
+    on_eng = [e for e in topo.engines(core, cores[partner]) if e not in off_eng]
+    me = host.index(r)
+
+    def near_index(q, s):
+        return [t for t in range(N) if topo.host(cores[t]) == topo.host(cores[q]) and t != q].index(s)
+
+    def dst(q):
+        rid, pid = topo.addr(cores[q], core)
+        return [DstId(rid=rid, pnc=pid)]
+
+    sent = [0]
+
+    def fused(parts):
+        ts = []
+        for q, eng, s, src, d in parts:
+            ts.append(RemoteDMATransfer(dst_ids=dst(q), dma_engine_mask=bits(eng), remote_sem=s, src=src, dst=d))
+            sent[0] += len(eng)
+        g.remote_dma_fused(ts, local_sem=sem.sent)
+
+    def u8(x):
+        return x.bitcast(dt.uint8)
+
+    two = len(off_eng) // len(far)
+    four = len(off_eng) // len(mates)
+    feng = {q: off_eng[two * i:two * i + two] for i, q in enumerate(far)}
+    neng = {q: off_eng[four * i:four * i + four] for i, q in enumerate(mates)}
+    neng[partner] = on_eng
+
+    for k in range(4):
+        sy.dma_start(T.wl[16 * k:16 * k + 16, :], T.want[:]).then_inc(sem.want, 16)
+    for k in range(4, 8):
+        a.dma_start(T.wl[16 * k:16 * k + 16, :], T.want[:]).then_inc(sem.want, 16)
+    sy.dma_start(T.xt[:], T.x[:]).then_inc(sem.xl, 16)
+    for k in range(8):
+        sy.dma_start(T.ol[16 * k:16 * k + 16, :], T.own[:]).then_inc(sem.own, 16)
+    for k in range(8):
+        sy.dma_start(T.sl[16 * k:16 * k + 16, :], T.slot[:]).then_inc(sem.slot, 16)
+    sy.dma_start(T.wt[:], T.w[:]).then_inc(sem.wl, 16)
+
+    g.wait_ge(sem.want, 128)
+
+    def wslice(q):
+        return T.wl[:, 3 * q:3 * q + 3]
+
+    fused([(q, feng[q], sem.lf, wslice(q), T.lf[:, 3 * me:3 * me + 3]) for q in far])
+
+    def nlist(q):
+        k = near_index(q, r)
+        return (q, neng[q], sem.ln, wslice(q), T.ln[:, 3 * k:3 * k + 3])
+
+    fused([nlist(q) for q in mates])
+    fused([nlist(partner)])
+    g.wait_ge(sem.e1, 1)
+    g.affine_select(T.e2[:], T.e1[:], [[-1, 520]], AluOpType.is_equal, 0.0, 3, 4).then_inc(sem.e2, 1)
+
+    g.wait_ge(sem.qf, 1)
+
+    def cols(q, eng, buf, i, land, s):
+        c, d = CAPP * i, CAPP * me
+        return [(q, eng, s, u8(T[buf][:, c:c + CAPP]), u8(T[land][:, d:d + CAPP])),
+                (q, eng, s, T[buf + "s"][:, c:c + CAPP], T[land + "s"][:, d:d + CAPP])]
+
+    fc = [cols(q, feng[q], "qf", i, "cf", sem.cf) for i, q in enumerate(far)]
+    fused([p[0] for p in fc])
+    fused([p[1] for p in fc])
+    g.wait_ge(sem.qn, 1)
+    nc = [cols(q, neng[q], "qn", i, "cn", sem.cn) for i, q in enumerate(near)]
+    fused([p[0] for p in nc])
+    fused([p[1] for p in nc])
+
+    def mout(lo, hi, scales):
+        if scales:
+            s, i, o = T.ms[:, lo:hi], T.is_[:, lo:hi], T.os_[:, lo:hi]
+        else:
+            s, i, o = u8(T.mq[:, lo:hi]), u8(T.iq[:, lo:hi]), u8(T.oq[:, lo:hi])
+        fused([(away, off_eng, sem.mo, s, o), (partner, on_eng, sem.mi, s, i)])
+
+    g.wait_ge(sem.q0, 1)
+    mout(0, H, False)
+    g.wait_ge(sem.q1, 1)
+    mout(H, S, False)
+    mout(0, S, True)
+    g.wait_ge(sem.sent, sent[0])
+
+    def sgather(out, off, t, scale=None):
+        w = T.xt[:, t:4 * XC].indirect(off)
+        if scale is None:
+            return a.activation(out, w, COPY)
+        return a.activation(out, w, COPY, scale=scale)
+
+    a.wait_ge(sem.xl, 16)
+    a.wait_ge(sem.cvf, 1)
+    for t in (2, 3):
+        sgather(T.hf[:, t:768:4], T.fo[:, 0:12], t).then_inc(sem.gfs, 1)
+    a.wait_ge(sem.cvn, 1)
+    for t in (2, 3):
+        sgather(T.hn[:, t:576:4], T.no[:, 0:9], t).then_inc(sem.gns, 1)
+    a.wait_ge(sem.hoz, 1)
+    a.wait_ge(sem.cvw, 1)
+    for t in range(4):
+        sgather(T.ho[:, t:192:4], T.wo[:, 0:3], t).then_inc(sem.gos, 1)
+    a.wait_ge(sem.cvo, 1)
+    for t in range(4):
+        sgather(T.xo[:, S * t:S * t + S], T.oo[:, 0:16], t, 0.5).then_inc(sem["xo%d" % t], 1)
+
+    def window(b, grp):
+        base = N * CAPP * b + CAPP * grp[0]
+        return T.dw[:, base:base + CAPP * G]
+
+    for b in (0, 2):
+        a.wait_ge(sem["df%d" % b], 1)
+        a.activation(window(b, far), T.pf[:, 512 * b:512 * b + 192], COPY).then_inc(sem["wf%d" % b], 1)
+    for b in range(4):
+        a.wait_ge(sem["dn%d" % b], 1)
+        a.activation(window(b, host), T.pn[:, 512 * b:512 * b + 192], COPY).then_inc(sem["wn%d" % b], 1)
+    a.wait_ge(sem.po, 1)
+    a.activation(T.yo[:], T.pf[:, 0:S], COPY).then_inc(sem.yo, 1)
+    a.wait_ge(sem.pf1, 1)
+    a.activation(T.yf[:, H:S], T.pf[:, 1536:1536 + H], COPY).then_inc(sem.yf1, 1)
+    slot_i, slot_o = (0, 2) if partner == left else (2, 0)
+    a.wait_ge(sem.yf1, 1)
+    a.dma_start(T.y[:, S * slot_o + H:S * slot_o + S], T.yf[:, H:S]).then_inc(sem.st2, 16)
+    a.wait_ge(sem.st2, 16)
+
+    sy.wait_ge(sem.qo, 1)
+    sy.dma_start(u8(T.cn[:, CAPP * me:CAPP * me + CAPP]), u8(T.qo[:, 0:CAPP])).then_inc(sem.oc, 16)
+    sy.dma_start(T.cns[:, CAPP * me:CAPP * me + CAPP], T.qos[:, 0:CAPP]).then_inc(sem.oc, 16)
+    sy.wait_ge(sem.yo, 1)
+    sy.dma_start(T.y[:, S:2 * S], T.yo[:]).then_inc(sem.st1, 16)
+    sy.wait_ge(sem.yi, 1)
+    sy.dma_start(T.y[:, S * slot_i:S * slot_i + S], T.yi[:]).then_inc(sem.st1, 16)
+    sy.wait_ge(sem.yf0, 1)
+    sy.dma_start(T.y[:, S * slot_o:S * slot_o + H], T.yf[:, 0:H]).then_inc(sem.st1, 16)
+    sy.wait_ge(sem.st1, 48)
+
+    v.memset(T.e1[:], 0.5).then_inc(sem.e1, 1)
+    v.memset(T.ho[:], 0.0).then_inc(sem.hoz, 1)
+    v.wait_ge(sem.want, 128)
+
+    def conv(out, in_, mul, s):
+        v.tensor_scalar(out, in_, mul, None, AluOpType.mult).then_inc(s, 1)
+
+    conv(T.wo[:, 0:3], wslice(r), 4.0, sem.cvw)
+
+    def vgather(out, off, t, s):
+        v.tensor_copy(out, T.xt[:, t:4 * XC].indirect(off)).then_inc(s, 1)
+
+    v.wait_ge(sem.lf, two * len(far))
+    conv(T.fo[:], T.lf[:], 4.0, sem.cvf)
+    v.wait_ge(sem.cvf, 1)
+    v.wait_ge(sem.xl, 16)
+    for t in (0, 1):
+        vgather(T.hf[:, t:768:4], T.fo[:, 0:12], t, sem.gfv)
+    v.wait_ge(sem.gfv, 2)
+    v.wait_ge(sem.gfs, 2)
+    v.quantize_mx(T.qf[:], T.qfs[:], T.hf[:]).then_inc(sem.qf, 1)
+    v.wait_ge(sem.ln, sum(len(neng[q]) for q in near))
+    conv(T.no[:, 0:9], T.ln[:, 0:9], 4.0, sem.cvn)
+    v.wait_ge(sem.cvn, 1)
+    for t in (0, 1):
+        vgather(T.hn[:, t:576:4], T.no[:, 0:9], t, sem.gnv)
+    v.wait_ge(sem.gnv, 2)
+    v.wait_ge(sem.gns, 2)
+    v.quantize_mx(T.qn[:], T.qns[:], T.hn[:]).then_inc(sem.qn, 1)
+    v.wait_ge(sem.own, 128)
+    conv(T.oo[:], T.ol[:], 4.0, sem.cvo)
+    v.wait_ge(sem.slot, 128)
+    conv(T.so[:], T.sl[:], 1.0, sem.cvs)
+    v.wait_ge(sem.gos, 4)
+    v.quantize_mx(T.qo[:], T.qos[:], T.ho[:]).then_inc(sem.qo, 1)
+    v.wait_ge(sem.e2, 1)
+    for b in range(4):
+        v.quantize_mx(T.eq[:, 128 * b:128 * b + 128], T.es[:, 128 * b:128 * b + 128],
+                      T.e2[:, 3 - b:3 - b + 512]).then_inc(sem.eq, 1)
+    v.wait_ge(sem.wl, 16)
+    v.quantize_mx(T.wq[:], T.ws[:], T.wt[:]).then_inc(sem.wq, 1)
+    for b in (1, 3):
+        v.wait_ge(sem["df%d" % b], 1)
+        v.tensor_copy(window(b, far), T.pf[:, 512 * b:512 * b + 192]).then_inc(sem["wf%d" % b], 1)
+    v.wait_ge(sem.cvs, 1)
+
+    def half(b, h):
+        v.tensor_tensor(T.m[:, 4 * H * h + b:4 * H * (h + 1):4],
+                        T.dw[:, N * CAPP * b:N * CAPP * (b + 1)].indirect(T.so[:, 8 * h:8 * h + 8]),
+                        T.xo[:, S * b + H * h:S * b + H * h + H], AluOpType.add).then_inc(sem["ga%d" % h], 1)
+
+    for b in range(4):
+        v.wait_ge(sem["xo%d" % b], 1)
+        v.wait_ge(sem["wf%d" % b], 1)
+        v.wait_ge(sem["wn%d" % b], 1)
+        half(b, 0)
+        if b == 0:
+            half(b, 1)
+    v.wait_ge(sem.ga0, 4)
+    v.quantize_mx(T.mq[:, 0:H], T.ms[:, 0:H], T.m[:, 0:4 * H]).then_inc(sem.q0, 1)
+    for b in range(1, 4):
+        half(b, 1)
+    v.wait_ge(sem.ga1, 4)
+    v.quantize_mx(T.mq[:, H:S], T.ms[:, H:S], T.m[:, 4 * H:4 * S]).then_inc(sem.q1, 1)
+    v.wait_ge(sem.pi, 1)
+    v.tensor_copy(T.yi[:], T.pf[:, 512:512 + S]).then_inc(sem.yi, 1)
+    v.wait_ge(sem.pf0, 1)
+    v.tensor_copy(T.yf[:, 0:H], T.pf[:, 1024:1024 + H]).then_inc(sem.yf0, 1)
+
+    def mm(out, l, ls, x, xs, s):
+        pe.matmul_mx(out, l, ls, x, xs, True, True).then_inc(s, 1)
+
+    def decode(p, c, cs, d):
+        for b in range(4):
+            mm(T[p][:, 512 * b:512 * b + 192], T.eq[:, 128 * b:128 * b + 128], T.es[:, 128 * b:128 * b + 128],
+               T[c][:], T[cs][:], sem["%s%d" % (d, b)])
+
+    pe.wait_ge(sem.eq, 4)
+    pe.wait_ge(sem.cf, 2 * two * len(far))
+    decode("pf", "cf", "cfs", "df")
+    pe.wait_ge(sem.oc, 32)
+    pe.wait_ge(sem.cn, 2 * sum(len(neng[q]) for q in near))
+    decode("pn", "cn", "cns", "dn")
+    pe.wait_ge(sem.wq, 1)
+    pe.wait_ge(sem.q0, 1)
+    pe.wait_ge(sem.q1, 1)
+    mm(T.pf[:, 0:S], T.wq[:], T.ws[:], T.mq[:], T.ms[:], sem.po)
+    pe.wait_ge(sem.mi, 3 * len(on_eng))
+    mm(T.pf[:, 512:512 + S], T.wq[:], T.ws[:], T.iq[:], T.is_[:], sem.pi)
+    pe.wait_ge(sem.mo, 3 * len(off_eng))
+    mm(T.pf[:, 1024:1024 + H], T.wq[:], T.ws[:], T.oq[:, 0:H], T.os_[:, 0:H], sem.pf0)
+    mm(T.pf[:, 1536:1536 + H], T.wq[:], T.ws[:], T.oq[:, H:S], T.os_[:, H:S], sem.pf1)

@@ -1,43 +1,47 @@
-from concourse.bass import DstId, RemoteDMATransfer, IndirectOffsetOnAxis
+from concourse.bass import DstId, RemoteDMATransfer
 from concourse.mybir import dt, AluOpType, ActivationFunctionType
 
 N, CAPP, S, XC = 8, 48, 256, 512
-G = 4
 H = S // 2
+C = CAPP
+Q = 128
 
 SCRATCH = {
     "wl": ("sbuf", [128, 24], "int32"),
     "ol": ("sbuf", [128, 16], "int32"),
-    "sl": ("sbuf", [128, 16], "int32"),
-    "lf": ("sbuf", [128, 12], "int32"),
-    "ln": ("sbuf", [128, 12], "int32"),
-    "fo": ("sbuf", [128, 12], "uint16"),
-    "no": ("sbuf", [128, 16], "uint16"),
-    "wo": ("sbuf", [128, 8], "uint16"),
+    "sl": ("sbuf", [128, 16 * N], "int32"),
+    "s2": ("sbuf", [128, 64], "int32"),
+    "s3": ("sbuf", [128, 32], "int32"),
+    "s4": ("sbuf", [128, 16], "int32"),
+    "wo": ("sbuf", [128, 24], "uint16"),
+    "l0": ("sbuf", [128, 8], "uint16"),
+    "l1": ("sbuf", [128, 8], "uint16"),
+    "l2": ("sbuf", [128, 16], "uint16"),
+    "l3": ("sbuf", [128, 8], "uint16"),
     "oo": ("sbuf", [128, 16], "uint16"),
     "so": ("sbuf", [128, 16], "uint16"),
     "xt": ("sbuf", [128, 4 * XC], "bfloat16"),
     "wt": ("sbuf", [128, 512], "bfloat16"),
     "wq": ("sbuf", [128, 128], "float8_e4m3fn_x4"),
     "ws": ("sbuf", [128, 128], "uint8"),
-    "e1": ("sbuf", [128, 520], "bfloat16"),
+    "e1": ("sbuf", [128, 128], "bfloat16"),
     "e2": ("sbuf", [128, 520], "bfloat16"),
     "eq": ("sbuf", [128, 512], "float8_e4m3fn_x4"),
     "es": ("sbuf", [128, 512], "uint8"),
-    "hf": ("sbuf", [128, 4 * 192], "bfloat16"),
-    "hn": ("sbuf", [128, 4 * 144], "bfloat16"),
-    "ho": ("sbuf", [128, 512], "bfloat16"),
-    "qf": ("sbuf", [128, 192], "float8_e4m3fn_x4"),
-    "qfs": ("sbuf", [128, 192], "uint8"),
-    "qn": ("sbuf", [128, 144], "float8_e4m3fn_x4"),
-    "qns": ("sbuf", [128, 144], "uint8"),
-    "qo": ("sbuf", [128, 128], "float8_e4m3fn_x4"),
-    "qos": ("sbuf", [128, 128], "uint8"),
-    "cf": ("sbuf", [128, 192], "float8_e4m3fn_x4"),
-    "cfs": ("sbuf", [128, 192], "uint8"),
-    "cn": ("sbuf", [128, 192], "float8_e4m3fn_x4"),
-    "cns": ("sbuf", [128, 192], "uint8"),
-    "dw": ("sbuf", [128, 4 * N * CAPP], "float32"),
+    "h1": ("sbuf", [128, 4 * 3 * C], "bfloat16"),
+    "h2": ("sbuf", [128, 4 * 3 * C], "bfloat16"),
+    "h3": ("sbuf", [128, 4 * Q], "bfloat16"),
+    "c1": ("sbuf", [128, 5 * C], "float8_e4m3fn_x4"),
+    "c1s": ("sbuf", [128, 5 * C], "uint8"),
+    "c2": ("sbuf", [128, 3 * C], "float8_e4m3fn_x4"),
+    "c2s": ("sbuf", [128, 3 * C], "uint8"),
+    "q2": ("sbuf", [128, 3 * C], "float8_e4m3fn_x4"),
+    "q2s": ("sbuf", [128, 3 * C], "uint8"),
+    "q3": ("sbuf", [128, Q], "float8_e4m3fn_x4"),
+    "q3s": ("sbuf", [128, Q], "uint8"),
+    "c3": ("sbuf", [128, 3 * C], "float8_e4m3fn_x4"),
+    "c3s": ("sbuf", [128, 3 * C], "uint8"),
+    "dw": ("sbuf", [128, 4 * N * C], "float32"),
     "xo": ("sbuf", [128, 4 * S], "float32"),
     "m": ("sbuf", [128, 4 * S], "bfloat16"),
     "mq": ("sbuf", [128, S], "float8_e4m3fn_x4"),
@@ -46,18 +50,15 @@ SCRATCH = {
     "is_": ("sbuf", [128, S], "uint8"),
     "oq": ("sbuf", [128, S], "float8_e4m3fn_x4"),
     "os_": ("sbuf", [128, S], "uint8"),
-    "yo": ("sbuf", [128, S], "float32"),
-    "yi": ("sbuf", [128, S], "float32"),
-    "yf": ("sbuf", [128, S], "float32"),
+    "yt": ("sbuf", [128, 3 * S], "float32"),
     "pf": ("psum", [128, 2048], "float32"),
     "pn": ("psum", [128, 2048], "float32"),
 }
-SEMAPHORES = (["want", "xl", "own", "slot", "wl", "sent", "lf", "ln", "cf", "cn", "mi", "mo", "e1", "e2", "eq", "wq",
-               "hoz", "cvw", "cvo", "cvs", "cvf", "cvn", "gfv", "gfs", "gnv", "gns", "gos", "qf", "qn", "qo", "oc", "q0", "q1",
-               "yo", "yi", "yf0", "yf1", "po", "pi", "pf0", "pf1", "st1", "st2"]
-              + ["df%d" % b for b in range(4)] + ["dn%d" % b for b in range(4)]
-              + ["wf%d" % b for b in range(4)] + ["wn%d" % b for b in range(4)]
-              + ["xo%d" % b for b in range(4)] + ["ga0", "ga1"])
+SEMAPHORES = (["want", "xl", "own", "slot", "wl", "sent", "sent3", "l1", "l2", "l3", "ca", "cb", "cl",
+               "mi0", "mi1", "mo0", "mo1", "e1", "e2", "eq", "wq", "cw", "c0", "co", "r1", "r2", "r3", "r4", "cs",
+               "v1", "v2", "v3", "a1", "a2", "a3", "q1", "q2", "q3", "m0", "m1", "ga0", "ga1", "st1", "st2"]
+              + ["%s%d" % (s, b) for s in ("da", "db", "dl", "wa", "wb", "wc", "xo") for b in range(4)]
+              + ["%s%d" % (s, k) for s in ("p", "y") for k in range(5)])
 
 
 def bits(engines):
@@ -74,240 +75,230 @@ def rank_program(g, core, T, topo):
     sem = T.sem
     v, a, pe, sy = g.vector, g.scalar, g.tensor, g.sync
     COPY = ActivationFunctionType.Copy
+    MUL, ADD = AluOpType.mult, AluOpType.add
     cores = T.cores
 
-    host = [q for q in range(N) if topo.host(cores[q]) == topo.host(core)]
-    far = [q for q in range(N) if q not in host]
-    near = [q for q in host if q != r]
-    mates = [q for q in near if topo.mates(core, cores[q])]
-    partner = [q for q in near if q not in mates][0]
+    def same_die(q):
+        return topo.die(cores[q]) == topo.die(core)
+
+    def by_die(chip):
+        return [q for q in chip if same_die(q)][0], [q for q in chip if not same_die(q)][0]
+
+    far = [q for q in range(N) if topo.host(cores[q]) != topo.host(core)]
+    a_rel, a_par = by_die([q for q in far if not topo.same_plane(core, cores[q])])
+    b_rel, b_par = by_die([q for q in far if topo.same_plane(core, cores[q])])
+    mates = [q for q in range(N) if topo.mates(core, cores[q])]
+    chip = [q for q in range(N) if cores[q] in topo.cores_of(core)]
+    partner = [q for q in chip if q != r][0]
     left, right = (r - 1) % N, (r + 1) % N
     away = left if right == partner else right
-    off_eng = topo.engines(core, cores[far[0]])
+    off_eng = topo.engines(core, cores[a_rel])
     on_eng = [e for e in topo.engines(core, cores[partner]) if e not in off_eng]
-    me = host.index(r)
+    no, ni = len(off_eng), len(on_eng)
+    half_eng = (off_eng[:no // 2], off_eng[no // 2:])
+    arrival = [r, a_rel, partner, b_par, b_rel, a_par] + mates
 
-    def near_index(q, s):
-        return [t for t in range(N) if topo.host(cores[t]) == topo.host(cores[q]) and t != q].index(s)
+    sent = {"sent": 0, "sent3": 0}
 
-    def dst(q):
-        rid, pid = topo.addr(cores[q], core)
-        return [DstId(rid=rid, pnc=pid)]
-
-    sent = [0]
-
-    def fused(parts):
+    def fused(parts, local="sent"):
         ts = []
         for q, eng, s, src, d in parts:
-            ts.append(RemoteDMATransfer(dst_ids=dst(q), dma_engine_mask=bits(eng), remote_sem=s, src=src, dst=d))
-            sent[0] += len(eng)
-        g.remote_dma_fused(ts, local_sem=sem.sent)
+            rid, pid = topo.addr(cores[q], core)
+            ts.append(RemoteDMATransfer(dst_ids=[DstId(rid=rid, pnc=pid)], dma_engine_mask=bits(eng), remote_sem=s,
+                                        src=src, dst=d))
+            sent[local] += len(eng)
+        g.remote_dma_fused(ts, local_sem=sem[local])
 
     def u8(x):
         return x.bitcast(dt.uint8)
 
-    two = len(off_eng) // len(far)
-    four = len(off_eng) // len(mates)
-    feng = {q: off_eng[two * i:two * i + two] for i, q in enumerate(far)}
-    neng = {q: off_eng[four * i:four * i + four] for i, q in enumerate(mates)}
-    neng[partner] = on_eng
+    def send(parts, local="sent"):
+        fused([(q, e, s, u8(src[0][:, i:i + n]), u8(d[0][:, j:j + n])) for q, e, s, src, i, d, j, n in parts], local)
+        fused([(q, e, s, src[1][:, i:i + n], d[1][:, j:j + n]) for q, e, s, src, i, d, j, n in parts], local)
 
-    for k in range(4):
-        sy.dma_start(T.wl[16 * k:16 * k + 16, :], T.want[:]).then_inc(sem.want, 16)
-    for k in range(4, 8):
-        a.dma_start(T.wl[16 * k:16 * k + 16, :], T.want[:]).then_inc(sem.want, 16)
+    c1, q2, c2, q3, c3 = (T.c1, T.c1s), (T.q2, T.q2s), (T.c2, T.c2s), (T.q3, T.q3s), (T.c3, T.c3s)
+    mq, iq, oq = (T.mq, T.ms), (T.iq, T.is_), (T.oq, T.os_)
+
+    sy.dma_start(T.wl[0:16, :], T.want[:]).then_inc(sem.want, 16)
+    a.dma_start(T.wl[16:32, :], T.want[:]).then_inc(sem.want, 16)
     sy.dma_start(T.xt[:], T.x[:]).then_inc(sem.xl, 16)
-    for k in range(8):
-        sy.dma_start(T.ol[16 * k:16 * k + 16, :], T.own[:]).then_inc(sem.own, 16)
-    for k in range(8):
-        sy.dma_start(T.sl[16 * k:16 * k + 16, :], T.slot[:]).then_inc(sem.slot, 16)
-    sy.dma_start(T.wt[:], T.w[:]).then_inc(sem.wl, 16)
+    for k in range(2):
+        a.dma_start(T.ol[16 * k:16 * k + 16, :], T.own[:]).then_inc(sem.own, 16)
+    for k in range(2):
+        a.dma_start(T.sl[16 * k:16 * k + 16, 0:16], T.slot[:]).then_inc(sem.slot, 16)
 
-    g.wait_ge(sem.want, 128)
+    g.wait_ge(sem.e1, 3)
+    g.affine_select(T.e2[:, 3:3 + 512:4], T.e1[:], [[-1, 128]], AluOpType.is_equal, 0.0, 0, 1).then_inc(sem.e2, 1)
+    g.wait_ge(sem.cw, 4)
 
-    def wslice(q):
-        return T.wl[:, 3 * q:3 * q + 3]
+    def lst(q, eng, land, k):
+        return (q, eng, sem[land], T.wo[:, 3 * q:3 * q + 3], T[land][:, 3 * k:3 * k + 3])
 
-    fused([(q, feng[q], sem.lf, wslice(q), T.lf[:, 3 * me:3 * me + 3]) for q in far])
-
-    def nlist(q):
-        k = near_index(q, r)
-        return (q, neng[q], sem.ln, wslice(q), T.ln[:, 3 * k:3 * k + 3])
-
-    fused([nlist(q) for q in mates])
-    fused([nlist(partner)])
-    g.wait_ge(sem.e1, 1)
-    g.affine_select(T.e2[:], T.e1[:], [[-1, 520]], AluOpType.is_equal, 0.0, 3, 4).then_inc(sem.e2, 1)
-
-    g.wait_ge(sem.qf, 1)
-
-    def cols(q, eng, buf, i, land, s):
-        c, d = CAPP * i, CAPP * me
-        return [(q, eng, s, u8(T[buf][:, c:c + CAPP]), u8(T[land][:, d:d + CAPP])),
-                (q, eng, s, T[buf + "s"][:, c:c + CAPP], T[land + "s"][:, d:d + CAPP])]
-
-    fc = [cols(q, feng[q], "qf", i, "cf", sem.cf) for i, q in enumerate(far)]
-    fused([p[0] for p in fc])
-    fused([p[1] for p in fc])
-    g.wait_ge(sem.qn, 1)
-    nc = [cols(q, neng[q], "qn", i, "cn", sem.cn) for i, q in enumerate(near)]
-    fused([p[0] for p in nc])
-    fused([p[1] for p in nc])
-
-    def mout(lo, hi, scales):
-        if scales:
-            s, i, o = T.ms[:, lo:hi], T.is_[:, lo:hi], T.os_[:, lo:hi]
-        else:
-            s, i, o = u8(T.mq[:, lo:hi]), u8(T.iq[:, lo:hi]), u8(T.oq[:, lo:hi])
-        fused([(away, off_eng, sem.mo, s, o), (partner, on_eng, sem.mi, s, i)])
-
-    g.wait_ge(sem.q0, 1)
-    mout(0, H, False)
+    fused([lst(a_rel, half_eng[0], "l1", 0), lst(a_par, half_eng[1], "l1", 1)])
+    fused([lst(b_rel, half_eng[0], "l2", 2), lst(b_par, half_eng[1], "l2", 1), lst(partner, on_eng, "l2", 0)])
+    fused([lst(q, half_eng[i], "l3", chip.index(r)) for i, q in enumerate(mates)])
     g.wait_ge(sem.q1, 1)
-    mout(H, S, False)
-    mout(0, S, True)
-    g.wait_ge(sem.sent, sent[0])
+    send([(a_rel, off_eng, sem.ca, c1, 0, c1, 3 * C, 2 * C)])
+    g.wait_ge(sem.q2, 1)
+    send([(b_par, half_eng[0], sem.cb, q2, C, c2, C, C), (b_rel, half_eng[1], sem.cb, q2, 2 * C, c2, 2 * C, C),
+          (partner, on_eng, sem.cb, q2, 0, c2, 0, C)])
+    g.wait_ge(sem.q3, 1)
+    send([(q, half_eng[i], sem.cl, q3, C * i, c3, C * (1 + chip.index(r)), C) for i, q in enumerate(mates)], "sent3")
+    g.wait_ge(sem.ca, 2 * no)
+    send([(partner, on_eng, sem.cl, c1, 4 * C, c3, 0, C)])
+    for h in range(2):
+        g.wait_ge(sem["m%d" % h], 1)
+        send([(away, off_eng, sem["mo%d" % h], mq, H * h, oq, H * h, H),
+              (partner, on_eng, sem["mi%d" % h], mq, H * h, iq, H * h, H)])
+    g.wait_ge(sem.sent, sent["sent"])
 
-    def sgather(out, off, t, scale=None):
-        w = T.xt[:, t:4 * XC].indirect(off)
-        if scale is None:
-            return a.activation(out, w, COPY)
-        return a.activation(out, w, COPY, scale=scale)
+    own_cols = (T.h1, 2 * C, C, T.l0)
+    groups = [(T.h1, 0, 2 * C, T.l1), (T.h2, 0, 3 * C, T.l2), (T.h3, 0, 2 * C, T.l3)]
+    lists_in = [no, no + ni, no]
+
+    def sides(grp, t):
+        h, c, n, off = grp
+        return h[:, 4 * c + t:4 * (c + n):4], T.xt[:, t:4 * XC].indirect(off[:, 0:n // 16])
+
+    def window(b, k, n):
+        return T.dw[:, N * C * b + C * k:N * C * b + C * (k + n)]
+
+    yi, yo = (0, 2 * S) if partner == left else (2 * S, 0)
+    res = [(T.pn[:, 0:S], S, S), (T.pn[:, 512:512 + H], yi, H), (T.pn[:, 1024:1024 + H], yo, H),
+           (T.pn[:, 1536:1536 + H], yi + H, H), (T.pf[:, 0:H], yo + H, H)]
+
+    def own_half(b):
+        a.activation(T.xo[:, S * b:S * b + S], T.xt[:, b:4 * XC].indirect(T.oo[:]), COPY, scale=0.5).then_inc(sem["xo%d" % b], 1)
 
     a.wait_ge(sem.xl, 16)
-    a.wait_ge(sem.cvf, 1)
+    a.wait_ge(sem.c0, 1)
     for t in (2, 3):
-        sgather(T.hf[:, t:768:4], T.fo[:, 0:12], t).then_inc(sem.gfs, 1)
-    a.wait_ge(sem.cvn, 1)
-    for t in (2, 3):
-        sgather(T.hn[:, t:576:4], T.no[:, 0:9], t).then_inc(sem.gns, 1)
-    a.wait_ge(sem.hoz, 1)
-    a.wait_ge(sem.cvw, 1)
-    for t in range(4):
-        sgather(T.ho[:, t:192:4], T.wo[:, 0:3], t).then_inc(sem.gos, 1)
-    a.wait_ge(sem.cvo, 1)
-    for t in range(4):
-        sgather(T.xo[:, S * t:S * t + S], T.oo[:, 0:16], t, 0.5).then_inc(sem["xo%d" % t], 1)
-
-    def window(b, grp):
-        base = N * CAPP * b + CAPP * grp[0]
-        return T.dw[:, base:base + CAPP * G]
-
-    for b in (0, 2):
-        a.wait_ge(sem["df%d" % b], 1)
-        a.activation(window(b, far), T.pf[:, 512 * b:512 * b + 192], COPY).then_inc(sem["wf%d" % b], 1)
+        a.activation(*sides(own_cols, t), COPY).then_inc(sem.a1, 1)
+    a.wait_ge(sem.co, 4)
+    own_half(0)
+    for k, grp in enumerate(groups):
+        a.wait_ge(sem["l%d" % (k + 1)], lists_in[k])
+        for t in (2, 3):
+            a.activation(*sides(grp, t), COPY).then_inc(sem["a%d" % (k + 1)], 1)
+    for b in range(1, 4):
+        own_half(b)
     for b in range(4):
-        a.wait_ge(sem["dn%d" % b], 1)
-        a.activation(window(b, host), T.pn[:, 512 * b:512 * b + 192], COPY).then_inc(sem["wn%d" % b], 1)
-    a.wait_ge(sem.po, 1)
-    a.activation(T.yo[:], T.pf[:, 0:S], COPY).then_inc(sem.yo, 1)
-    a.wait_ge(sem.pf1, 1)
-    a.activation(T.yf[:, H:S], T.pf[:, 1536:1536 + H], COPY).then_inc(sem.yf1, 1)
-    slot_i, slot_o = (0, 2) if partner == left else (2, 0)
-    a.wait_ge(sem.yf1, 1)
-    a.dma_start(T.y[:, S * slot_o + H:S * slot_o + S], T.yf[:, H:S]).then_inc(sem.st2, 16)
+        a.wait_ge(sem["da%d" % b], 1)
+        a.activation(window(b, 0, 2), T.pf[:, 512 * b:512 * b + 2 * C], COPY).then_inc(sem["wa%d" % b], 1)
+    for b in range(4):
+        a.wait_ge(sem["dl%d" % b], 1)
+        a.activation(window(b, 5, 3), T.pf[:, 512 * b:512 * b + 3 * C], COPY).then_inc(sem["wc%d" % b], 1)
+    for k in (0, 2, 4):
+        p, c, n = res[k]
+        a.wait_ge(sem["p%d" % k], 1)
+        a.activation(T.yt[:, c:c + n], p, COPY).then_inc(sem["y%d" % k], 1)
+    p, c, n = res[4]
+    a.wait_ge(sem.y4, 1)
+    a.dma_start(T.y[:, c:c + n], T.yt[:, c:c + n]).then_inc(sem.st2, 16)
     a.wait_ge(sem.st2, 16)
 
-    sy.wait_ge(sem.qo, 1)
-    sy.dma_start(u8(T.cn[:, CAPP * me:CAPP * me + CAPP]), u8(T.qo[:, 0:CAPP])).then_inc(sem.oc, 16)
-    sy.dma_start(T.cns[:, CAPP * me:CAPP * me + CAPP], T.qos[:, 0:CAPP]).then_inc(sem.oc, 16)
-    sy.wait_ge(sem.yo, 1)
-    sy.dma_start(T.y[:, S:2 * S], T.yo[:]).then_inc(sem.st1, 16)
-    sy.wait_ge(sem.yi, 1)
-    sy.dma_start(T.y[:, S * slot_i:S * slot_i + S], T.yi[:]).then_inc(sem.st1, 16)
-    sy.wait_ge(sem.yf0, 1)
-    sy.dma_start(T.y[:, S * slot_o:S * slot_o + H], T.yf[:, 0:H]).then_inc(sem.st1, 16)
-    sy.wait_ge(sem.st1, 48)
+    sy.wait_ge(sem.sent3, sent["sent3"])
+    sy.dma_start(T.wt[:], T.w[:]).then_inc(sem.wl, 16)
+    for k in range(4):
+        p, c, n = res[k]
+        sy.wait_ge(sem["y%d" % k], 1)
+        sy.dma_start(T.y[:, c:c + n], T.yt[:, c:c + n]).then_inc(sem.st1, 16)
+    sy.wait_ge(sem.st1, 64)
 
     v.memset(T.e1[:], 0.5).then_inc(sem.e1, 1)
-    v.memset(T.ho[:], 0.0).then_inc(sem.hoz, 1)
-    v.wait_ge(sem.want, 128)
+    v.memset(T.e2[:], 0.0).then_inc(sem.e1, 1)
+    v.memset(T.h3[:, 8 * C:4 * Q], 0.0).then_inc(sem.e1, 1)
 
-    def conv(out, in_, mul, s):
-        v.tensor_scalar(out, in_, mul, None, AluOpType.mult).then_inc(s, 1)
+    def spread(out, in_, num, op, s):
+        for k in range(4):
+            v.tensor_scalar(out[32 * k:32 * k + 32, :], in_, num, None, op).then_inc(s, 1)
 
-    conv(T.wo[:, 0:3], wslice(r), 4.0, sem.cvw)
-
-    def vgather(out, off, t, s):
-        v.tensor_copy(out, T.xt[:, t:4 * XC].indirect(off)).then_inc(s, 1)
-
-    v.wait_ge(sem.lf, two * len(far))
-    conv(T.fo[:], T.lf[:], 4.0, sem.cvf)
-    v.wait_ge(sem.cvf, 1)
-    v.wait_ge(sem.xl, 16)
-    for t in (0, 1):
-        vgather(T.hf[:, t:768:4], T.fo[:, 0:12], t, sem.gfv)
-    v.wait_ge(sem.gfv, 2)
-    v.wait_ge(sem.gfs, 2)
-    v.quantize_mx(T.qf[:], T.qfs[:], T.hf[:]).then_inc(sem.qf, 1)
-    v.wait_ge(sem.ln, sum(len(neng[q]) for q in near))
-    conv(T.no[:, 0:9], T.ln[:, 0:9], 4.0, sem.cvn)
-    v.wait_ge(sem.cvn, 1)
-    for t in (0, 1):
-        vgather(T.hn[:, t:576:4], T.no[:, 0:9], t, sem.gnv)
-    v.wait_ge(sem.gnv, 2)
-    v.wait_ge(sem.gns, 2)
-    v.quantize_mx(T.qn[:], T.qns[:], T.hn[:]).then_inc(sem.qn, 1)
-    v.wait_ge(sem.own, 128)
-    conv(T.oo[:], T.ol[:], 4.0, sem.cvo)
-    v.wait_ge(sem.slot, 128)
-    conv(T.so[:], T.sl[:], 1.0, sem.cvs)
-    v.wait_ge(sem.gos, 4)
-    v.quantize_mx(T.qo[:], T.qos[:], T.ho[:]).then_inc(sem.qo, 1)
+    v.wait_ge(sem.want, 32)
+    spread(T.wo, T.wl[0:32, :], 4.0, MUL, sem.cw)
+    v.wait_ge(sem.cw, 4)
+    v.tensor_copy(T.l0[:, 0:3], T.wo[:, 3 * r:3 * r + 3]).then_inc(sem.c0, 1)
     v.wait_ge(sem.e2, 1)
     for b in range(4):
         v.quantize_mx(T.eq[:, 128 * b:128 * b + 128], T.es[:, 128 * b:128 * b + 128],
                       T.e2[:, 3 - b:3 - b + 512]).then_inc(sem.eq, 1)
-    v.wait_ge(sem.wl, 16)
-    v.quantize_mx(T.wq[:], T.ws[:], T.wt[:]).then_inc(sem.wq, 1)
-    for b in (1, 3):
-        v.wait_ge(sem["df%d" % b], 1)
-        v.tensor_copy(window(b, far), T.pf[:, 512 * b:512 * b + 192]).then_inc(sem["wf%d" % b], 1)
-    v.wait_ge(sem.cvs, 1)
+    v.wait_ge(sem.own, 32)
+    spread(T.oo, T.ol[0:32, :], 4.0, MUL, sem.co)
+    v.wait_ge(sem.xl, 16)
+    v.wait_ge(sem.c0, 1)
+    for t in (0, 1):
+        v.tensor_copy(*sides(own_cols, t)).then_inc(sem.v1, 1)
+    outs = [(T.c1[:, 0:3 * C], T.c1s[:, 0:3 * C]), (T.q2[:], T.q2s[:]), (T.q3[:], T.q3s[:])]
+    for k, grp in enumerate(groups):
+        v.wait_ge(sem["l%d" % (k + 1)], lists_in[k])
+        for t in (0, 1):
+            v.tensor_copy(*sides(grp, t)).then_inc(sem["v%d" % (k + 1)], 1)
+        v.wait_ge(sem["v%d" % (k + 1)], 4 if k == 0 else 2)
+        v.wait_ge(sem["a%d" % (k + 1)], 4 if k == 0 else 2)
+        v.quantize_mx(outs[k][0], outs[k][1], grp[0][:]).then_inc(sem["q%d" % (k + 1)], 1)
+
+    shift = [C * (arrival.index(q) - q) for q in range(N)]
+    v.wait_ge(sem.slot, 32)
+    for q in range(1, N):
+        v.tensor_scalar(T.sl[0:32, 16 * q:16 * q + 16], T.sl[0:32, 0:16], float(C * q), float(shift[q] - shift[q - 1]),
+                        AluOpType.is_ge, MUL).then_inc(sem.r1, 1)
+    v.wait_ge(sem.r1, N - 1)
+    for src, out, n, s in ((T.sl, T.s2, 64, sem.r2), (T.s2, T.s3, 32, sem.r3), (T.s3, T.s4, 16, sem.r4)):
+        v.tensor_tensor(out[0:32, :], src[0:32, 0:n], src[0:32, n:2 * n], ADD).then_inc(s, 1)
+        v.wait_ge(s, 1)
+    spread(T.so, T.s4[0:32, :], float(shift[0]), ADD, sem.cs)
+    for b in range(4):
+        v.wait_ge(sem["db%d" % b], 1)
+        v.tensor_copy(window(b, 2, 3), T.pn[:, 512 * b:512 * b + 3 * C]).then_inc(sem["wb%d" % b], 1)
+    v.wait_ge(sem.cs, 4)
 
     def half(b, h):
         v.tensor_tensor(T.m[:, 4 * H * h + b:4 * H * (h + 1):4],
-                        T.dw[:, N * CAPP * b:N * CAPP * (b + 1)].indirect(T.so[:, 8 * h:8 * h + 8]),
-                        T.xo[:, S * b + H * h:S * b + H * h + H], AluOpType.add).then_inc(sem["ga%d" % h], 1)
+                        T.dw[:, N * C * b:N * C * (b + 1)].indirect(T.so[:, 8 * h:8 * h + 8]),
+                        T.xo[:, S * b + H * h:S * b + H * h + H], ADD).then_inc(sem["ga%d" % h], 1)
 
     for b in range(4):
-        v.wait_ge(sem["xo%d" % b], 1)
-        v.wait_ge(sem["wf%d" % b], 1)
-        v.wait_ge(sem["wn%d" % b], 1)
+        for s in ("xo", "wa", "wb", "wc"):
+            v.wait_ge(sem["%s%d" % (s, b)], 1)
         half(b, 0)
         if b == 0:
             half(b, 1)
     v.wait_ge(sem.ga0, 4)
-    v.quantize_mx(T.mq[:, 0:H], T.ms[:, 0:H], T.m[:, 0:4 * H]).then_inc(sem.q0, 1)
+    v.quantize_mx(T.mq[:, 0:H], T.ms[:, 0:H], T.m[:, 0:4 * H]).then_inc(sem.m0, 1)
     for b in range(1, 4):
         half(b, 1)
     v.wait_ge(sem.ga1, 4)
-    v.quantize_mx(T.mq[:, H:S], T.ms[:, H:S], T.m[:, 4 * H:4 * S]).then_inc(sem.q1, 1)
-    v.wait_ge(sem.pi, 1)
-    v.tensor_copy(T.yi[:], T.pf[:, 512:512 + S]).then_inc(sem.yi, 1)
-    v.wait_ge(sem.pf0, 1)
-    v.tensor_copy(T.yf[:, 0:H], T.pf[:, 1024:1024 + H]).then_inc(sem.yf0, 1)
+    v.quantize_mx(T.mq[:, H:S], T.ms[:, H:S], T.m[:, 4 * H:4 * S]).then_inc(sem.m1, 1)
+    v.wait_ge(sem.wl, 16)
+    v.quantize_mx(T.wq[:], T.ws[:], T.wt[:]).then_inc(sem.wq, 1)
+    for k in (1, 3):
+        p, c, n = res[k]
+        v.wait_ge(sem["p%d" % k], 1)
+        v.tensor_copy(T.yt[:, c:c + n], p).then_inc(sem["y%d" % k], 1)
 
-    def mm(out, l, ls, x, xs, s):
-        pe.matmul_mx(out, l, ls, x, xs, True, True).then_inc(s, 1)
+    def mm(out, l, ls, x, c, n, s):
+        pe.matmul_mx(out, l, ls, x[0][:, c:c + n], x[1][:, c:c + n], True, True).then_inc(s, 1)
 
-    def decode(p, c, cs, d):
+    def decode(p, x, c, n, d, after=None):
         for b in range(4):
-            mm(T[p][:, 512 * b:512 * b + 192], T.eq[:, 128 * b:128 * b + 128], T.es[:, 128 * b:128 * b + 128],
-               T[c][:], T[cs][:], sem["%s%d" % (d, b)])
+            if after:
+                pe.wait_ge(sem["%s%d" % (after, b)], 1)
+            mm(p[:, 512 * b:512 * b + n], T.eq[:, 128 * b:128 * b + 128], T.es[:, 128 * b:128 * b + 128],
+               x, c, n, sem["%s%d" % (d, b)])
 
     pe.wait_ge(sem.eq, 4)
-    pe.wait_ge(sem.cf, 2 * two * len(far))
-    decode("pf", "cf", "cfs", "df")
-    pe.wait_ge(sem.oc, 32)
-    pe.wait_ge(sem.cn, 2 * sum(len(neng[q]) for q in near))
-    decode("pn", "cn", "cns", "dn")
-    pe.wait_ge(sem.wq, 1)
-    pe.wait_ge(sem.q0, 1)
     pe.wait_ge(sem.q1, 1)
-    mm(T.pf[:, 0:S], T.wq[:], T.ws[:], T.mq[:], T.ms[:], sem.po)
-    pe.wait_ge(sem.mi, 3 * len(on_eng))
-    mm(T.pf[:, 512:512 + S], T.wq[:], T.ws[:], T.iq[:], T.is_[:], sem.pi)
-    pe.wait_ge(sem.mo, 3 * len(off_eng))
-    mm(T.pf[:, 1024:1024 + H], T.wq[:], T.ws[:], T.oq[:, 0:H], T.os_[:, 0:H], sem.pf0)
-    mm(T.pf[:, 1536:1536 + H], T.wq[:], T.ws[:], T.oq[:, H:S], T.os_[:, H:S], sem.pf1)
+    pe.wait_ge(sem.ca, 2 * no)
+    decode(T.pf, c1, 2 * C, Q, "da")
+    pe.wait_ge(sem.cb, 2 * ni + 2 * no)
+    decode(T.pn, c2, 0, 3 * C, "db")
+    pe.wait_ge(sem.cl, 2 * ni + 2 * no)
+    decode(T.pf, c3, 0, 3 * C, "dl", "wa")
+    pe.wait_ge(sem.wq, 1)
+    pe.wait_ge(sem.m0, 1)
+    pe.wait_ge(sem.m1, 1)
+    mm(res[0][0], T.wq[:], T.ws[:], mq, 0, S, sem.p0)
+    for h in range(2):
+        pe.wait_ge(sem["mi%d" % h], 2 * ni)
+        mm(res[1 + 2 * h][0], T.wq[:], T.ws[:], iq, H * h, H, sem["p%d" % (1 + 2 * h)])
+        pe.wait_ge(sem["mo%d" % h], 2 * no)
+        mm(res[2 + 2 * h][0], T.wq[:], T.ws[:], oq, H * h, H, sem["p%d" % (2 + 2 * h)])

@@ -2,24 +2,33 @@ from concourse.bass import DstId, RemoteDMATransfer
 from concourse.mybir import dt, AluOpType, ActivationFunctionType
 
 N, CAPP, S, XC = 8, 48, 256, 512
-H = S // 2
 C = CAPP
+W = N * C
 Q = 128
+PAD = Q - 2 * C
+ROW = XC // 16
+PIECES = [(0, 2, 0), (2, 3, 6), (5, 3, 16)]
 
 SCRATCH = {
     "wl": ("sbuf", [128, 24], "int32"),
     "ol": ("sbuf", [128, 16], "int32"),
-    "sl": ("sbuf", [128, 16 * N], "int32"),
-    "s2": ("sbuf", [128, 64], "int32"),
-    "s3": ("sbuf", [128, 32], "int32"),
-    "s4": ("sbuf", [128, 16], "int32"),
-    "wo": ("sbuf", [128, 24], "uint16"),
-    "l0": ("sbuf", [128, 8], "uint16"),
+    "sl": ("sbuf", [128, 16], "int32"),
+    "s1": ("sbuf", [128, 16], "int32"),
+    "s2": ("sbuf", [128, 16], "int32"),
+    "pi": ("sbuf", [128, 16], "int32"),
+    "po": ("sbuf", [128, 16], "uint16"),
+    "ov": ("sbuf", [128, 16], "uint16"),
+    "cn": ("sbuf", [128, XC], "float32"),
+    "val": ("sbuf", [128, S], "float32"),
+    "tb": ("sbuf", [128, ROW], "float32"),
+    "to": ("sbuf", [128, 26], "uint16"),
+    "wo": ("sbuf", [128, 26], "uint16"),
     "l1": ("sbuf", [128, 8], "uint16"),
     "l2": ("sbuf", [128, 16], "uint16"),
     "l3": ("sbuf", [128, 8], "uint16"),
-    "oo": ("sbuf", [128, 16], "uint16"),
     "so": ("sbuf", [128, 16], "uint16"),
+    "si": ("sbuf", [128, 16], "uint16"),
+    "sa": ("sbuf", [128, 16], "uint16"),
     "xt": ("sbuf", [128, 4 * XC], "bfloat16"),
     "wt": ("sbuf", [128, 512], "bfloat16"),
     "wq": ("sbuf", [128, 128], "float8_e4m3fn_x4"),
@@ -35,30 +44,29 @@ SCRATCH = {
     "c1s": ("sbuf", [128, 5 * C], "uint8"),
     "c2": ("sbuf", [128, 3 * C], "float8_e4m3fn_x4"),
     "c2s": ("sbuf", [128, 3 * C], "uint8"),
-    "q2": ("sbuf", [128, 3 * C], "float8_e4m3fn_x4"),
-    "q2s": ("sbuf", [128, 3 * C], "uint8"),
-    "q3": ("sbuf", [128, Q], "float8_e4m3fn_x4"),
-    "q3s": ("sbuf", [128, Q], "uint8"),
     "c3": ("sbuf", [128, 3 * C], "float8_e4m3fn_x4"),
-    "c3s": ("sbuf", [128, 3 * C], "uint8"),
-    "dw": ("sbuf", [128, 4 * N * C], "float32"),
-    "xo": ("sbuf", [128, 4 * S], "float32"),
-    "m": ("sbuf", [128, 4 * S], "bfloat16"),
-    "mq": ("sbuf", [128, S], "float8_e4m3fn_x4"),
-    "ms": ("sbuf", [128, S], "uint8"),
-    "iq": ("sbuf", [128, S], "float8_e4m3fn_x4"),
-    "is_": ("sbuf", [128, S], "uint8"),
-    "oq": ("sbuf", [128, S], "float8_e4m3fn_x4"),
-    "os_": ("sbuf", [128, S], "uint8"),
+    "c3s": ("sbuf", [128, 6 * C], "uint8"),
+    "xs": ("sbuf", [128, 4 * W], "float32"),
+    "m0": ("sbuf", [128, 4 * Q], "bfloat16"),
+    "m1": ("sbuf", [128, 4 * 3 * C], "bfloat16"),
+    "m2": ("sbuf", [128, 4 * 3 * C], "bfloat16"),
+    "mq": ("sbuf", [128, PAD + W], "float8_e4m3fn_x4"),
+    "ms": ("sbuf", [128, PAD + W], "uint8"),
+    "iq": ("sbuf", [128, Q + W], "float8_e4m3fn_x4"),
+    "is_": ("sbuf", [128, Q + W], "uint8"),
+    "oq": ("sbuf", [128, W + 3 * C], "float8_e4m3fn_x4"),
+    "os_": ("sbuf", [128, W + 3 * C], "uint8"),
+    "yw": ("sbuf", [128, 3 * W], "float32"),
     "yt": ("sbuf", [128, 3 * S], "float32"),
     "pf": ("psum", [128, 2048], "float32"),
     "pn": ("psum", [128, 2048], "float32"),
 }
-SEMAPHORES = (["want", "xl", "own", "slot", "wl", "sent", "sent3", "l1", "l2", "l3", "ca", "cb", "cl",
-               "mi0", "mi1", "mo0", "mo1", "e1", "e2", "eq", "wq", "cw", "c0", "co", "r1", "r2", "r3", "r4", "cs",
-               "v1", "v2", "v3", "a1", "a2", "a3", "q1", "q2", "q3", "m0", "m1", "ga0", "ga1", "st1", "st2"]
-              + ["%s%d" % (s, b) for s in ("da", "db", "dl", "wa", "wb", "wc", "xo") for b in range(4)]
-              + ["%s%d" % (s, k) for s in ("p", "y") for k in range(5)])
+SEMAPHORES = (["want", "xl", "own", "slot", "slot7", "wl", "tb", "sent", "po2", "ca", "cb", "cl", "ls", "e1", "e2", "z", "ip",
+               "cn", "wq", "cw", "co", "r1", "r2", "po", "val", "inv", "cs", "st1", "st2", "po0"]
+              + ["%s%d" % (s, k) for s in "lvaq" for k in (1, 2, 3)]
+              + ["%s%d" % (s, k) for s in ("t", "ad", "m", "mi", "ma", "pi", "pa") for k in range(3)]
+              + ["%s%s" % (s, who) for s in "ky" for who in "oia"] + ["eq%d" % b for b in range(4)]
+              + ["%s%d%d" % (s, k, b) for s in "dx" for k in range(3) for b in range(4)])
 
 
 def bits(engines):
@@ -66,6 +74,21 @@ def bits(engines):
     for e in engines:
         m |= 1 << e
     return m
+
+
+def places(T, topo, r):
+    cores = T.cores
+    core = cores[r]
+    mates = [q for q in range(N) if topo.mates(core, cores[q])]
+    relay = [q for q in mates if topo.die(cores[q]) == topo.die(core)][0]
+    beyond = [q for q in mates if q != relay][0]
+    far = [q for q in range(N) if topo.host(cores[q]) != topo.host(core)]
+    second = [q for q in far if topo.same_plane(core, cores[q])]
+    third = [q for q in far if not topo.same_plane(core, cores[q])]
+    chip = [q for q in range(N) if cores[q] in topo.cores_of(core)]
+    partner = [q for q in chip if q != r][0]
+    runs = [[r], [relay], [partner], second, [beyond], third]
+    return relay, beyond, second, third, partner, chip.index(r), runs
 
 
 def rank_program(g, core, T, topo):
@@ -78,25 +101,14 @@ def rank_program(g, core, T, topo):
     MUL, ADD = AluOpType.mult, AluOpType.add
     cores = T.cores
 
-    def same_die(q):
-        return topo.die(cores[q]) == topo.die(core)
-
-    def by_die(chip):
-        return [q for q in chip if same_die(q)][0], [q for q in chip if not same_die(q)][0]
-
-    far = [q for q in range(N) if topo.host(cores[q]) != topo.host(core)]
-    a_rel, a_par = by_die([q for q in far if not topo.same_plane(core, cores[q])])
-    b_rel, b_par = by_die([q for q in far if topo.same_plane(core, cores[q])])
-    mates = [q for q in range(N) if topo.mates(core, cores[q])]
-    chip = [q for q in range(N) if cores[q] in topo.cores_of(core)]
-    partner = [q for q in chip if q != r][0]
+    relay, beyond, second, third, partner, me, runs = places(T, topo, r)
     left, right = (r - 1) % N, (r + 1) % N
     away = left if right == partner else right
-    off_eng = topo.engines(core, cores[a_rel])
+    off_eng = topo.engines(core, cores[relay])
     on_eng = [e for e in topo.engines(core, cores[partner]) if e not in off_eng]
     no, ni = len(off_eng), len(on_eng)
-    half_eng = (off_eng[:no // 2], off_eng[no // 2:])
-    arrival = [r, a_rel, partner, b_par, b_rel, a_par] + mates
+    half_off = (off_eng[:no // 2], off_eng[no // 2:])
+    half_on = (on_eng[:ni // 2], on_eng[ni // 2:])
 
     sent = {"sent": 0, "sent3": 0}
 
@@ -114,191 +126,230 @@ def rank_program(g, core, T, topo):
 
     def send(parts, local="sent"):
         fused([(q, e, s, u8(src[0][:, i:i + n]), u8(d[0][:, j:j + n])) for q, e, s, src, i, d, j, n in parts], local)
-        fused([(q, e, s, src[1][:, i:i + n], d[1][:, j:j + n]) for q, e, s, src, i, d, j, n in parts], local)
+        fused([(q, e, s, src[1][:, i + src[2]:i + src[2] + n], d[1][:, j + d[2]:j + d[2] + n])
+               for q, e, s, src, i, d, j, n in parts], local)
 
-    c1, q2, c2, q3, c3 = (T.c1, T.c1s), (T.q2, T.q2s), (T.c2, T.c2s), (T.q3, T.q3s), (T.c3, T.c3s)
-    mq, iq, oq = (T.mq, T.ms), (T.iq, T.is_), (T.oq, T.os_)
+    c1, c2, c3 = (T.c1, T.c1s, 0), (T.c2, T.c2s, 0), (T.c3, T.c3s, 3 * C)
+    mq, iq, oq = (T.mq, T.ms, 0), (T.iq, T.is_, 0), (T.oq, T.os_, 0)
+    odd = 3 * r % 2
 
-    sy.dma_start(T.wl[0:16, :], T.want[:]).then_inc(sem.want, 16)
-    a.dma_start(T.wl[16:32, :], T.want[:]).then_inc(sem.want, 16)
+    def wanted(q):
+        return T.wo[:, odd + 3 * q:odd + 3 * q + 3]
+
+    for k, queue in enumerate((sy, a)):
+        queue.dma_start(T.wl[16 * k:16 * k + 16, :], T.want[:]).then_inc(sem.want, 16)
+    sy.dma_start(T.sl[0:16, :], T.slot[:]).then_inc(sem.slot, 16)
+    a.dma_start(T.ol[0:16, :], T.own[:]).then_inc(sem.own, 16)
     sy.dma_start(T.xt[:], T.x[:]).then_inc(sem.xl, 16)
-    for k in range(2):
-        a.dma_start(T.ol[16 * k:16 * k + 16, :], T.own[:]).then_inc(sem.own, 16)
-    for k in range(2):
-        a.dma_start(T.sl[16 * k:16 * k + 16, 0:16], T.slot[:]).then_inc(sem.slot, 16)
+    sy.dma_start(T.wt[:], T.w[:]).then_inc(sem.wl, 16)
+    for k in range(1, 8):
+        sy.dma_start(T.sl[16 * k:16 * k + 16, :], T.slot[:]).then_inc(sem.slot7, 16)
 
-    g.wait_ge(sem.e1, 3)
+    g.iota(T.pi[:], [[16, 16]], 0, 1).then_inc(sem.ip, 1)
+    g.iota(T.cn[:, 0:XC // 4], [[4, XC // 4]], 0, 0, allow_small_or_imprecise_dtypes=True).then_inc(sem.cn, 1)
+    g.wait_ge(sem.e1, 2)
     g.affine_select(T.e2[:, 3:3 + 512:4], T.e1[:], [[-1, 128]], AluOpType.is_equal, 0.0, 0, 1).then_inc(sem.e2, 1)
     g.wait_ge(sem.cw, 4)
 
     def lst(q, eng, land, k):
-        return (q, eng, sem[land], T.wo[:, 3 * q:3 * q + 3], T[land][:, 3 * k:3 * k + 3])
+        return (q, eng, sem[land], wanted(q), T[land][:, 3 * k:3 * k + 3])
 
-    fused([lst(a_rel, half_eng[0], "l1", 0), lst(a_par, half_eng[1], "l1", 1)])
-    fused([lst(b_rel, half_eng[0], "l2", 2), lst(b_par, half_eng[1], "l2", 1), lst(partner, on_eng, "l2", 0)])
-    fused([lst(q, half_eng[i], "l3", chip.index(r)) for i, q in enumerate(mates)])
+    fused([lst(relay, half_off[0], "l1", 0), lst(beyond, half_off[1], "l1", 1)])
+    fused([lst(q, half_off[i], "l2", 1 + me) for i, q in enumerate(second)])
+    fused([lst(q, half_off[i], "l3", me) for i, q in enumerate(third)] + [lst(partner, on_eng, "l2", 0)])
     g.wait_ge(sem.q1, 1)
-    send([(a_rel, off_eng, sem.ca, c1, 0, c1, 3 * C, 2 * C)])
+    send([(relay, off_eng, sem.ca, c1, 0, c1, 3 * C, 2 * C)])
     g.wait_ge(sem.q2, 1)
-    send([(b_par, half_eng[0], sem.cb, q2, C, c2, C, C), (b_rel, half_eng[1], sem.cb, q2, 2 * C, c2, 2 * C, C),
-          (partner, on_eng, sem.cb, q2, 0, c2, 0, C)])
+    send([(q, half_off[i], sem.cb, oq, W + C * (1 + i), c2, C * (1 + me), C) for i, q in enumerate(second)]
+         + [(partner, on_eng, sem.cb, oq, W, c2, 0, C)])
     g.wait_ge(sem.q3, 1)
-    send([(q, half_eng[i], sem.cl, q3, C * i, c3, C * (1 + chip.index(r)), C) for i, q in enumerate(mates)], "sent3")
+    send([(q, half_off[i], sem.cl, iq, C * i, c3, C * (1 + me), C) for i, q in enumerate(third)])
     g.wait_ge(sem.ca, 2 * no)
-    send([(partner, on_eng, sem.cl, c1, 4 * C, c3, 0, C)])
-    for h in range(2):
-        g.wait_ge(sem["m%d" % h], 1)
-        send([(away, off_eng, sem["mo%d" % h], mq, H * h, oq, H * h, H),
-              (partner, on_eng, sem["mi%d" % h], mq, H * h, iq, H * h, H)])
+    fused([(partner, half_on[0], sem.cl, u8(T.c1[:, 4 * C:5 * C]), u8(T.c3[:, 0:C])),
+           (partner, half_on[1], sem.cl, T.c1s[:, C:5 * C], T.c3s[:, 0:4 * C])])
+    g.wait_ge(sem.cs, 1)
+    fused([(away, off_eng, sem.ls, T.so[:], T.sa[:]), (partner, on_eng, sem.ls, T.so[:], T.si[:])])
+    for k, (first, n, o) in enumerate(PIECES):
+        g.wait_ge(sem["m%d" % k], 1)
+        send([(away, off_eng, sem["ma%d" % k], mq, PAD + C * first, oq, W - C * (first + n), C * n),
+              (partner, on_eng, sem["mi%d" % k], mq, PAD + C * first, iq, Q + C * first, C * n)])
     g.wait_ge(sem.sent, sent["sent"])
 
-    own_cols = (T.h1, 2 * C, C, T.l0)
-    groups = [(T.h1, 0, 2 * C, T.l1), (T.h2, 0, 3 * C, T.l2), (T.h3, 0, 2 * C, T.l3)]
+    own_cols = (T.h1, 2 * C, C, wanted(r))
+    groups = [(T.h1, 0, 2 * C, T.l1[:, 0:6]), (T.h2, 0, 3 * C, T.l2[:, 0:9]), (T.h3, 0, 2 * C, T.l3[:, 0:6])]
     lists_in = [no, no + ni, no]
+    by_vector = [2, 2, 1]
 
     def sides(grp, t):
         h, c, n, off = grp
-        return h[:, 4 * c + t:4 * (c + n):4], T.xt[:, t:4 * XC].indirect(off[:, 0:n // 16])
+        return h[:, 4 * c + t:4 * (c + n):4], T.xt[:, t:4 * XC].indirect(off)
 
-    def window(b, k, n):
-        return T.dw[:, N * C * b + C * k:N * C * b + C * (k + n)]
+    yi, ya = (0, 2) if partner == left else (2, 0)
+    prod = {"o": (r, T.so, 1), "i": (partner, T.si, yi), "a": (away, T.sa, ya)}
+    early = C * PIECES[2][0]
+    bank = {"o": [(T.pn, 1024, 1024), (T.pn, 1024, 1024 + C * PIECES[1][0]), (T.pf, 1536, 1536)],
+            "i": [(T.pn, 0, PAD), (T.pn, 1536, 1536), (T.pf, 512, 512)],
+            "a": [(T.pn, 512, 512), (T.pf, 0, 0), (T.pf, 1024, 1024)]}
 
-    yi, yo = (0, 2 * S) if partner == left else (2 * S, 0)
-    res = [(T.pn[:, 0:S], S, S), (T.pn[:, 512:512 + H], yi, H), (T.pn[:, 1024:1024 + H], yo, H),
-           (T.pn[:, 1536:1536 + H], yi + H, H), (T.pf[:, 0:H], yo + H, H)]
+    def to_slots(copy, who, k):
+        q, off, y = prod[who]
+        p, b, c = bank[who][k]
+        for run in places(T, topo, q)[6][2 * k:2 * k + 2]:
+            n = C * len(run)
+            copy(T.yw[:, W * y + C * run[0]:W * y + C * run[0] + n], p[:, c:c + n]).then_inc(sem["k" + who], 1)
+            c += n
 
-    def own_half(b):
-        a.activation(T.xo[:, S * b:S * b + S], T.xt[:, b:4 * XC].indirect(T.oo[:]), COPY, scale=0.5).then_inc(sem["xo%d" % b], 1)
+    def pick(queue, copy, who, lo=0, hi=S):
+        q, off, y = prod[who]
+        queue.wait_ge(sem["k" + who], len(runs))
+        copy(T.yt[:, S * y + lo:S * y + hi],
+             T.yw[:, W * y:W * y + W].indirect(off[:, lo // 16:hi // 16])).then_inc(sem["y" + who], 1)
 
+    def store(queue, who, s, picks=1):
+        y = prod[who][2]
+        queue.wait_ge(sem["y" + who], picks)
+        queue.dma_start(T.y[:, S * y:S * y + S], T.yt[:, S * y:S * y + S]).then_inc(s, 16)
+
+    def acopy(out, in_):
+        return a.activation(out, in_, COPY)
+
+    for k, n in enumerate((XC // 4, XC // 2)):
+        a.wait_ge(sem.cn, k + 1)
+        a.activation(T.cn[:, n:2 * n], T.cn[:, 0:n], ActivationFunctionType.Identity, bias=float(4 * n)).then_inc(sem.cn, 1)
+    a.wait_ge(sem.cn, 3)
+    a.wait_ge(sem.co, 1)
+    acopy(T.val[:], T.cn[:].indirect(T.ov[:])).then_inc(sem.val, 1)
     a.wait_ge(sem.xl, 16)
-    a.wait_ge(sem.c0, 1)
-    for t in (2, 3):
-        a.activation(*sides(own_cols, t), COPY).then_inc(sem.a1, 1)
-    a.wait_ge(sem.co, 4)
-    own_half(0)
+    a.wait_ge(sem.cw, 4)
+    for t in range(4):
+        acopy(*sides(own_cols, t)).then_inc(sem.a1, 1)
     for k, grp in enumerate(groups):
         a.wait_ge(sem["l%d" % (k + 1)], lists_in[k])
-        for t in (2, 3):
-            a.activation(*sides(grp, t), COPY).then_inc(sem["a%d" % (k + 1)], 1)
-    for b in range(1, 4):
-        own_half(b)
-    for b in range(4):
-        a.wait_ge(sem["da%d" % b], 1)
-        a.activation(window(b, 0, 2), T.pf[:, 512 * b:512 * b + 2 * C], COPY).then_inc(sem["wa%d" % b], 1)
-    for b in range(4):
-        a.wait_ge(sem["dl%d" % b], 1)
-        a.activation(window(b, 5, 3), T.pf[:, 512 * b:512 * b + 3 * C], COPY).then_inc(sem["wc%d" % b], 1)
-    for k in (0, 2, 4):
-        p, c, n = res[k]
-        a.wait_ge(sem["p%d" % k], 1)
-        a.activation(T.yt[:, c:c + n], p, COPY).then_inc(sem["y%d" % k], 1)
-    p, c, n = res[4]
-    a.wait_ge(sem.y4, 1)
-    a.dma_start(T.y[:, c:c + n], T.yt[:, c:c + n]).then_inc(sem.st2, 16)
+        for t in range(by_vector[k], 4):
+            acopy(*sides(grp, t)).then_inc(sem["a%d" % (k + 1)], 1)
+    for k, (first, n, o) in enumerate(PIECES):
+        a.wait_ge(sem["t%d" % k], 2)
+        for b in range(4):
+            c = W * b + C * first
+            a.activation(T.xs[:, c:c + C * n], T.xt[:, b:4 * XC].indirect(T.to[:, o:o + 3 * n]), COPY,
+                         scale=0.5).then_inc(sem["x%d%d" % (k, b)], 1)
+    a.wait_ge(sem.pa0, 1)
+    to_slots(acopy, "a", 0)
+    a.wait_ge(sem.cs, 1)
+    pick(a, acopy, "o")
+    for k in (1, 2):
+        a.wait_ge(sem["pa%d" % k], 1)
+        to_slots(acopy, "a", k)
+    a.wait_ge(sem.ls, no + ni)
+    pick(a, acopy, "a", 0, S // 2)
+    store(a, "a", sem.st2, 2)
     a.wait_ge(sem.st2, 16)
 
-    sy.wait_ge(sem.sent3, sent["sent3"])
-    sy.dma_start(T.wt[:], T.w[:]).then_inc(sem.wl, 16)
-    for k in range(4):
-        p, c, n = res[k]
-        sy.wait_ge(sem["y%d" % k], 1)
-        sy.dma_start(T.y[:, c:c + n], T.yt[:, c:c + n]).then_inc(sem.st1, 16)
-    sy.wait_ge(sem.st1, 64)
+    sy.wait_ge(sem.inv, 1)
+    sy.dma_start(T.tb[:], T.cn[0:8, :]).then_inc(sem.tb, 16)
+    store(sy, "o", sem.st1)
+    store(sy, "i", sem.st1)
+    sy.wait_ge(sem.st1, 32)
+
+    def quantise_constants(bb):
+        for b in bb:
+            v.quantize_mx(T.eq[:, 128 * b:128 * b + 128], T.es[:, 128 * b:128 * b + 128],
+                          T.e2[:, 3 - b:3 - b + 512]).then_inc(sem["eq%d" % b], 1)
 
     v.memset(T.e1[:], 0.5).then_inc(sem.e1, 1)
     v.memset(T.e2[:], 0.0).then_inc(sem.e1, 1)
-    v.memset(T.h3[:, 8 * C:4 * Q], 0.0).then_inc(sem.e1, 1)
-
-    def spread(out, in_, num, op, s):
-        for k in range(4):
-            v.tensor_scalar(out[32 * k:32 * k + 32, :], in_, num, None, op).then_inc(s, 1)
-
+    for z in (T.ov[:], T.h3[:, 8 * C:4 * Q], T.m0[:, 0:4 * PAD]):
+        v.memset(z, 0).then_inc(sem.z, 1)
+    v.wait_ge(sem.ip, 1)
+    v.tensor_copy(T.po[:], T.pi[:]).then_inc(sem.z, 1)
+    v.wait_ge(sem.z, 4)
     v.wait_ge(sem.want, 32)
-    spread(T.wo, T.wl[0:32, :], 4.0, MUL, sem.cw)
-    v.wait_ge(sem.cw, 4)
-    v.tensor_copy(T.l0[:, 0:3], T.wo[:, 3 * r:3 * r + 3]).then_inc(sem.c0, 1)
+    for k in range(4):
+        v.tensor_scalar(T.wo[32 * k:32 * k + 32, odd:odd + 24], T.wl[0:32, :], 4.0, None, MUL).then_inc(sem.cw, 1)
+    v.wait_ge(sem.own, 16)
+    v.tensor_copy(T.ov[0:16, :], T.ol[0:16, :]).then_inc(sem.co, 1)
+    v.wait_ge(sem.slot, 16)
+    v.tensor_scalar(T.s1[0:16, :], T.sl[0:16, :], float(16 * ROW + 1), None, MUL).then_inc(sem.r1, 1)
+    v.wait_ge(sem.r1, 1)
+    v.tensor_scalar(T.s2[0:16, :], T.s1[0:16, :], 4, 16 * ROW - 1, AluOpType.logical_shift_right,
+                    AluOpType.bitwise_and).then_inc(sem.r2, 1)
+    v.wait_ge(sem.r2, 1)
+    v.tensor_copy(T.po[0:16, :], T.s2[0:16, :]).then_inc(sem.po, 1)
     v.wait_ge(sem.e2, 1)
-    for b in range(4):
-        v.quantize_mx(T.eq[:, 128 * b:128 * b + 128], T.es[:, 128 * b:128 * b + 128],
-                      T.e2[:, 3 - b:3 - b + 512]).then_inc(sem.eq, 1)
-    v.wait_ge(sem.own, 32)
-    spread(T.oo, T.ol[0:32, :], 4.0, MUL, sem.co)
+    quantise_constants([0])
+    v.wait_ge(sem.po, 1)
+    v.wait_ge(sem.val, 1)
+    v.tensor_copy(T.cn[:].indirect(T.po[:]), T.val[:]).then_inc(sem.inv, 1)
     v.wait_ge(sem.xl, 16)
-    v.wait_ge(sem.c0, 1)
-    for t in (0, 1):
-        v.tensor_copy(*sides(own_cols, t)).then_inc(sem.v1, 1)
-    outs = [(T.c1[:, 0:3 * C], T.c1s[:, 0:3 * C]), (T.q2[:], T.q2s[:]), (T.q3[:], T.q3s[:])]
+    outs = [(T.c1[:, 0:3 * C], T.c1s[:, 0:3 * C]), (T.oq[:, W:W + 3 * C], T.os_[:, W:W + 3 * C]), (T.iq[:, 0:Q], T.is_[:, 0:Q])]
     for k, grp in enumerate(groups):
         v.wait_ge(sem["l%d" % (k + 1)], lists_in[k])
-        for t in (0, 1):
+        for t in range(by_vector[k]):
             v.tensor_copy(*sides(grp, t)).then_inc(sem["v%d" % (k + 1)], 1)
-        v.wait_ge(sem["v%d" % (k + 1)], 4 if k == 0 else 2)
-        v.wait_ge(sem["a%d" % (k + 1)], 4 if k == 0 else 2)
+        if k == 2:
+            v.wait_ge(sem.slot7, 112)
+            v.tensor_copy(T.so[:], T.sl[:]).then_inc(sem.cs, 1)
+        v.wait_ge(sem["v%d" % (k + 1)], by_vector[k])
+        v.wait_ge(sem["a%d" % (k + 1)], 4 - by_vector[k] + (4 if k == 0 else 0))
         v.quantize_mx(outs[k][0], outs[k][1], grp[0][:]).then_inc(sem["q%d" % (k + 1)], 1)
-
-    shift = [C * (arrival.index(q) - q) for q in range(N)]
-    v.wait_ge(sem.slot, 32)
-    for q in range(1, N):
-        v.tensor_scalar(T.sl[0:32, 16 * q:16 * q + 16], T.sl[0:32, 0:16], float(C * q), float(shift[q] - shift[q - 1]),
-                        AluOpType.is_ge, MUL).then_inc(sem.r1, 1)
-    v.wait_ge(sem.r1, N - 1)
-    for src, out, n, s in ((T.sl, T.s2, 64, sem.r2), (T.s2, T.s3, 32, sem.r3), (T.s3, T.s4, 16, sem.r4)):
-        v.tensor_tensor(out[0:32, :], src[0:32, 0:n], src[0:32, n:2 * n], ADD).then_inc(s, 1)
-        v.wait_ge(s, 1)
-    spread(T.so, T.s4[0:32, :], float(shift[0]), ADD, sem.cs)
-    for b in range(4):
-        v.wait_ge(sem["db%d" % b], 1)
-        v.tensor_copy(window(b, 2, 3), T.pn[:, 512 * b:512 * b + 3 * C]).then_inc(sem["wb%d" % b], 1)
-    v.wait_ge(sem.cs, 4)
-
-    def half(b, h):
-        v.tensor_tensor(T.m[:, 4 * H * h + b:4 * H * (h + 1):4],
-                        T.dw[:, N * C * b:N * C * (b + 1)].indirect(T.so[:, 8 * h:8 * h + 8]),
-                        T.xo[:, S * b + H * h:S * b + H * h + H], ADD).then_inc(sem["ga%d" % h], 1)
-
-    for b in range(4):
-        for s in ("xo", "wa", "wb", "wc"):
-            v.wait_ge(sem["%s%d" % (s, b)], 1)
-        half(b, 0)
-        if b == 0:
-            half(b, 1)
-    v.wait_ge(sem.ga0, 4)
-    v.quantize_mx(T.mq[:, 0:H], T.ms[:, 0:H], T.m[:, 0:4 * H]).then_inc(sem.m0, 1)
-    for b in range(1, 4):
-        half(b, 1)
-    v.wait_ge(sem.ga1, 4)
-    v.quantize_mx(T.mq[:, H:S], T.ms[:, H:S], T.m[:, 4 * H:4 * S]).then_inc(sem.m1, 1)
-    v.wait_ge(sem.wl, 16)
-    v.quantize_mx(T.wq[:], T.ws[:], T.wt[:]).then_inc(sem.wq, 1)
-    for k in (1, 3):
-        p, c, n = res[k]
-        v.wait_ge(sem["p%d" % k], 1)
-        v.tensor_copy(T.yt[:, c:c + n], p).then_inc(sem["y%d" % k], 1)
+    v.wait_ge(sem.tb, 16)
+    for k, (first, n, o) in enumerate(PIECES):
+        for run in runs[2 * k:2 * k + 2]:
+            v.tensor_copy(T.to[:, o:o + 3 * len(run)], T.tb[:, 3 * run[0]:3 * (run[-1] + 1)]).then_inc(sem["t%d" % k], 1)
+            o += 3 * len(run)
+        if k == 0:
+            quantise_constants([1, 2, 3])
+    banks = [T.pf, T.pn, T.pf]
+    for k, (first, n, o) in enumerate(PIECES):
+        m, pad = T["m%d" % k], PAD if k == 0 else 0
+        for b in range(4):
+            v.wait_ge(sem["d%d%d" % (k, b)], 1)
+            v.wait_ge(sem["x%d%d" % (k, b)], 1)
+            c = W * b + C * first
+            v.tensor_tensor(m[:, 4 * pad + b:4 * (pad + C * n):4], banks[k][:, 512 * b:512 * b + C * n],
+                            T.xs[:, c:c + C * n], ADD).then_inc(sem["ad%d" % k], 1)
+        v.wait_ge(sem["ad%d" % k], 4)
+        c = PAD + C * first
+        v.quantize_mx(T.mq[:, c - pad:c + C * n], T.ms[:, c - pad:c + C * n], m[:]).then_inc(sem["m%d" % k], 1)
+        if k == 0:
+            v.wait_ge(sem.wl, 16)
+            v.quantize_mx(T.wq[:], T.ws[:], T.wt[:]).then_inc(sem.wq, 1)
+    for k in range(3):
+        v.wait_ge(sem["po%d" % (k // 2 * 2)], 1)
+        to_slots(v.tensor_copy, "o", k)
+    for k in range(3):
+        v.wait_ge(sem["pi%d" % k], 1)
+        to_slots(v.tensor_copy, "i", k)
+    v.wait_ge(sem.ls, no + ni)
+    pick(v, v.tensor_copy, "i")
+    pick(v, v.tensor_copy, "a", S // 2, S)
 
     def mm(out, l, ls, x, c, n, s):
-        pe.matmul_mx(out, l, ls, x[0][:, c:c + n], x[1][:, c:c + n], True, True).then_inc(s, 1)
+        pe.matmul_mx(out, l, ls, x[0][:, c:c + n], x[1][:, c + x[2]:c + x[2] + n], True, True).then_inc(s, 1)
 
-    def decode(p, x, c, n, d, after=None):
+    def decode(k, x, c, n):
         for b in range(4):
-            if after:
-                pe.wait_ge(sem["%s%d" % (after, b)], 1)
-            mm(p[:, 512 * b:512 * b + n], T.eq[:, 128 * b:128 * b + 128], T.es[:, 128 * b:128 * b + 128],
-               x, c, n, sem["%s%d" % (d, b)])
+            pe.wait_ge(sem["eq%d" % b], 1)
+            mm(banks[k][:, 512 * b:512 * b + n], T.eq[:, 128 * b:128 * b + 128], T.es[:, 128 * b:128 * b + 128],
+               x, c, n, sem["d%d%d" % (k, b)])
 
-    pe.wait_ge(sem.eq, 4)
     pe.wait_ge(sem.q1, 1)
     pe.wait_ge(sem.ca, 2 * no)
-    decode(T.pf, c1, 2 * C, Q, "da")
+    decode(0, c1, 2 * C, Q)
     pe.wait_ge(sem.cb, 2 * ni + 2 * no)
-    decode(T.pn, c2, 0, 3 * C, "db")
-    pe.wait_ge(sem.cl, 2 * ni + 2 * no)
-    decode(T.pf, c3, 0, 3 * C, "dl", "wa")
-    pe.wait_ge(sem.wq, 1)
-    pe.wait_ge(sem.m0, 1)
-    pe.wait_ge(sem.m1, 1)
-    mm(res[0][0], T.wq[:], T.ws[:], mq, 0, S, sem.p0)
-    for h in range(2):
-        pe.wait_ge(sem["mi%d" % h], 2 * ni)
-        mm(res[1 + 2 * h][0], T.wq[:], T.ws[:], iq, H * h, H, sem["p%d" % (1 + 2 * h)])
-        pe.wait_ge(sem["mo%d" % h], 2 * no)
-        mm(res[2 + 2 * h][0], T.wq[:], T.ws[:], oq, H * h, H, sem["p%d" % (2 + 2 * h)])
+    decode(1, c2, 0, 3 * C)
+    pe.wait_ge(sem.cl, ni + 2 * no)
+    pe.wait_ge(sem.ad0, 4)
+    decode(2, c3, 0, 3 * C)
+    for s in ("wq", "q2", "q3", "m0", "m1"):
+        pe.wait_ge(sem[s], 1)
+    mm(T.pn[:, 1024:1024 + early], T.wq[:], T.ws[:], mq, PAD, early, sem.po0)
+    for k, (first, n, o) in enumerate(PIECES):
+        pad = max(0, Q - C * n)
+        for who, x, c, count in (("i", iq, Q + C * first - pad, 2 * ni), ("a", oq, W - C * (first + n), 2 * no)):
+            p, b, c0 = bank[who][k]
+            pe.wait_ge(sem["m%s%d" % (who, k)], count)
+            mm(p[:, b:b + C * n + pad], T.wq[:], T.ws[:], x, c, C * n + pad, sem["p%s%d" % (who, k)])
+        if k == 0:
+            pe.wait_ge(sem.m2, 1)
+            mm(T.pf[:, 1536:1536 + W - early], T.wq[:], T.ws[:], mq, PAD + early, W - early, sem.po2)

from concourse.bass import DstId, RemoteDMATransfer
from concourse.mybir import dt, AluOpType, ActivationFunctionType

N, CAPP, S, XC = 8, 48, 256, 512
C = CAPP
W = N * C
Q = 128
PAD = Q - 2 * C
ROW = XC // 16
PIECES = [(0, 2, 0), (2, 3, 6), (5, 3, 16)]

SCRATCH = {
    "wl": ("sbuf", [128, 24], "int32"),
    "ol": ("sbuf", [128, 16], "int32"),
    "sl": ("sbuf", [128, 16], "int32"),
    "s1": ("sbuf", [128, 16], "int32"),
    "s2": ("sbuf", [128, 16], "int32"),
    "pi": ("sbuf", [128, 16], "int32"),
    "po": ("sbuf", [128, 16], "uint16"),
    "ov": ("sbuf", [128, 16], "uint16"),
    "cn": ("sbuf", [128, XC], "float32"),
    "val": ("sbuf", [128, S], "float32"),
    "tb": ("sbuf", [128, ROW], "float32"),
    "to": ("sbuf", [128, 26], "uint16"),
    "wo": ("sbuf", [128, 26], "uint16"),
    "l1": ("sbuf", [128, 8], "uint16"),
    "l2": ("sbuf", [128, 16], "uint16"),
    "l3": ("sbuf", [128, 8], "uint16"),
    "so": ("sbuf", [128, 16], "uint16"),
    "si": ("sbuf", [128, 16], "uint16"),
    "sa": ("sbuf", [128, 16], "uint16"),
    "xt": ("sbuf", [128, 4 * XC], "bfloat16"),
    "wt": ("sbuf", [128, 512], "bfloat16"),
    "wq": ("sbuf", [128, 128], "float8_e4m3fn_x4"),
    "ws": ("sbuf", [128, 128], "uint8"),
    "e1": ("sbuf", [128, 128], "bfloat16"),
    "e2": ("sbuf", [128, 520], "bfloat16"),
    "eq": ("sbuf", [128, 512], "float8_e4m3fn_x4"),
    "es": ("sbuf", [128, 512], "uint8"),
    "h1": ("sbuf", [128, 4 * 3 * C], "bfloat16"),
    "h2": ("sbuf", [128, 4 * 3 * C], "bfloat16"),
    "h3": ("sbuf", [128, 4 * Q], "bfloat16"),
    "c1": ("sbuf", [128, 5 * C], "float8_e4m3fn_x4"),
    "c1s": ("sbuf", [128, 5 * C], "uint8"),
    "c2": ("sbuf", [128, 3 * C], "float8_e4m3fn_x4"),
    "c2s": ("sbuf", [128, 3 * C], "uint8"),
    "c3": ("sbuf", [128, 3 * C], "float8_e4m3fn_x4"),
    "c3s": ("sbuf", [128, 6 * C], "uint8"),
    "xs": ("sbuf", [128, 4 * W], "float32"),
    "m0": ("sbuf", [128, 4 * Q], "bfloat16"),
    "m1": ("sbuf", [128, 4 * 3 * C], "bfloat16"),
    "m2": ("sbuf", [128, 4 * 3 * C], "bfloat16"),
    "mq": ("sbuf", [128, PAD + W], "float8_e4m3fn_x4"),
    "ms": ("sbuf", [128, PAD + W], "uint8"),
    "iq": ("sbuf", [128, Q + W], "float8_e4m3fn_x4"),
    "is_": ("sbuf", [128, Q + W], "uint8"),
    "oq": ("sbuf", [128, W + 3 * C], "float8_e4m3fn_x4"),
    "os_": ("sbuf", [128, W + 3 * C], "uint8"),
    "yw": ("sbuf", [128, 3 * W], "float32"),
    "yt": ("sbuf", [128, 3 * S], "float32"),
    "pf": ("psum", [128, 2048], "float32"),
    "pn": ("psum", [128, 2048], "float32"),
}
SEMAPHORES = (["want", "xl", "own", "slot", "slot7", "wl", "tb", "sent", "po2", "ca", "cb", "cl", "ls", "e1", "e2", "z", "ip",
               "cn", "wq", "cw", "co", "r1", "r2", "po", "val", "inv", "cs", "st1", "st2", "po0"]
              + ["%s%d" % (s, k) for s in "lvaq" for k in (1, 2, 3)]
              + ["%s%d" % (s, k) for s in ("t", "ad", "m", "mi", "ma", "pi", "pa") for k in range(3)]
              + ["%s%s" % (s, who) for s in "ky" for who in "oia"] + ["eq%d" % b for b in range(4)]
              + ["%s%d%d" % (s, k, b) for s in "dx" for k in range(3) for b in range(4)])


def bits(engines):
    m = 0
    for e in engines:
        m |= 1 << e
    return m


def places(T, topo, r):
    cores = T.cores
    core = cores[r]
    mates = [q for q in range(N) if topo.mates(core, cores[q])]
    relay = [q for q in mates if topo.die(cores[q]) == topo.die(core)][0]
    beyond = [q for q in mates if q != relay][0]
    far = [q for q in range(N) if topo.host(cores[q]) != topo.host(core)]
    second = [q for q in far if topo.same_plane(core, cores[q])]
    third = [q for q in far if not topo.same_plane(core, cores[q])]
    chip = [q for q in range(N) if cores[q] in topo.cores_of(core)]
    partner = [q for q in chip if q != r][0]
    runs = [[r], [relay], [partner], second, [beyond], third]
    return relay, beyond, second, third, partner, chip.index(r), runs


def rank_program(g, core, T, topo):
    r = T.rank_of(core)
    if r is None:
        return
    sem = T.sem
    v, a, pe, sy = g.vector, g.scalar, g.tensor, g.sync
    COPY = ActivationFunctionType.Copy
    MUL, ADD = AluOpType.mult, AluOpType.add
    cores = T.cores

    relay, beyond, second, third, partner, me, runs = places(T, topo, r)
    left, right = (r - 1) % N, (r + 1) % N
    away = left if right == partner else right
    off_eng = topo.engines(core, cores[relay])
    on_eng = [e for e in topo.engines(core, cores[partner]) if e not in off_eng]
    no, ni = len(off_eng), len(on_eng)
    half_off = (off_eng[:no // 2], off_eng[no // 2:])
    half_on = (on_eng[:ni // 2], on_eng[ni // 2:])

    sent = {"sent": 0, "sent3": 0}

    def fused(parts, local="sent"):
        ts = []
        for q, eng, s, src, d in parts:
            rid, pid = topo.addr(cores[q], core)
            ts.append(RemoteDMATransfer(dst_ids=[DstId(rid=rid, pnc=pid)], dma_engine_mask=bits(eng), remote_sem=s,
                                        src=src, dst=d))
            sent[local] += len(eng)
        g.remote_dma_fused(ts, local_sem=sem[local])

    def u8(x):
        return x.bitcast(dt.uint8)

    def send(parts, local="sent"):
        fused([(q, e, s, u8(src[0][:, i:i + n]), u8(d[0][:, j:j + n])) for q, e, s, src, i, d, j, n in parts], local)
        fused([(q, e, s, src[1][:, i + src[2]:i + src[2] + n], d[1][:, j + d[2]:j + d[2] + n])
               for q, e, s, src, i, d, j, n in parts], local)

    c1, c2, c3 = (T.c1, T.c1s, 0), (T.c2, T.c2s, 0), (T.c3, T.c3s, 3 * C)
    mq, iq, oq = (T.mq, T.ms, 0), (T.iq, T.is_, 0), (T.oq, T.os_, 0)
    odd = 3 * r % 2

    def wanted(q):
        return T.wo[:, odd + 3 * q:odd + 3 * q + 3]

    for k, queue in enumerate((sy, a)):
        queue.dma_start(T.wl[16 * k:16 * k + 16, :], T.want[:]).then_inc(sem.want, 16)
    sy.dma_start(T.sl[0:16, :], T.slot[:]).then_inc(sem.slot, 16)
    a.dma_start(T.ol[0:16, :], T.own[:]).then_inc(sem.own, 16)
    sy.dma_start(T.xt[:], T.x[:]).then_inc(sem.xl, 16)
    sy.dma_start(T.wt[:], T.w[:]).then_inc(sem.wl, 16)
    for k in range(1, 8):
        sy.dma_start(T.sl[16 * k:16 * k + 16, :], T.slot[:]).then_inc(sem.slot7, 16)

    g.iota(T.pi[:], [[16, 16]], 0, 1).then_inc(sem.ip, 1)
    g.iota(T.cn[:, 0:XC // 4], [[4, XC // 4]], 0, 0, allow_small_or_imprecise_dtypes=True).then_inc(sem.cn, 1)
    g.wait_ge(sem.e1, 2)
    g.affine_select(T.e2[:, 3:3 + 512:4], T.e1[:], [[-1, 128]], AluOpType.is_equal, 0.0, 0, 1).then_inc(sem.e2, 1)
    g.wait_ge(sem.cw, 4)

    def lst(q, eng, land, k):
        return (q, eng, sem[land], wanted(q), T[land][:, 3 * k:3 * k + 3])

    fused([lst(relay, half_off[0], "l1", 0), lst(beyond, half_off[1], "l1", 1)])
    fused([lst(q, half_off[i], "l2", 1 + me) for i, q in enumerate(second)])
    fused([lst(q, half_off[i], "l3", me) for i, q in enumerate(third)] + [lst(partner, on_eng, "l2", 0)])
    g.wait_ge(sem.q1, 1)
    send([(relay, off_eng, sem.ca, c1, 0, c1, 3 * C, 2 * C)])
    g.wait_ge(sem.q2, 1)
    send([(q, half_off[i], sem.cb, oq, W + C * (1 + i), c2, C * (1 + me), C) for i, q in enumerate(second)]
         + [(partner, on_eng, sem.cb, oq, W, c2, 0, C)])
    g.wait_ge(sem.q3, 1)
    send([(q, half_off[i], sem.cl, iq, C * i, c3, C * (1 + me), C) for i, q in enumerate(third)])
    g.wait_ge(sem.ca, 2 * no)
    fused([(partner, half_on[0], sem.cl, u8(T.c1[:, 4 * C:5 * C]), u8(T.c3[:, 0:C])),
           (partner, half_on[1], sem.cl, T.c1s[:, C:5 * C], T.c3s[:, 0:4 * C])])
    g.wait_ge(sem.cs, 1)
    fused([(away, off_eng, sem.ls, T.so[:], T.sa[:]), (partner, on_eng, sem.ls, T.so[:], T.si[:])])
    for k, (first, n, o) in enumerate(PIECES):
        g.wait_ge(sem["m%d" % k], 1)
        send([(away, off_eng, sem["ma%d" % k], mq, PAD + C * first, oq, W - C * (first + n), C * n),
              (partner, on_eng, sem["mi%d" % k], mq, PAD + C * first, iq, Q + C * first, C * n)])
    g.wait_ge(sem.sent, sent["sent"])

    own_cols = (T.h1, 2 * C, C, wanted(r))
    groups = [(T.h1, 0, 2 * C, T.l1[:, 0:6]), (T.h2, 0, 3 * C, T.l2[:, 0:9]), (T.h3, 0, 2 * C, T.l3[:, 0:6])]
    lists_in = [no, no + ni, no]
    by_vector = [2, 2, 1]

    def sides(grp, t):
        h, c, n, off = grp
        return h[:, 4 * c + t:4 * (c + n):4], T.xt[:, t:4 * XC].indirect(off)

    yi, ya = (0, 2) if partner == left else (2, 0)
    prod = {"o": (r, T.so, 1), "i": (partner, T.si, yi), "a": (away, T.sa, ya)}
    early = C * PIECES[2][0]
    bank = {"o": [(T.pn, 1024, 1024), (T.pn, 1024, 1024 + C * PIECES[1][0]), (T.pf, 1536, 1536)],
            "i": [(T.pn, 0, PAD), (T.pn, 1536, 1536), (T.pf, 512, 512)],
            "a": [(T.pn, 512, 512), (T.pf, 0, 0), (T.pf, 1024, 1024)]}

    def to_slots(copy, who, k):
        q, off, y = prod[who]
        p, b, c = bank[who][k]
        for run in places(T, topo, q)[6][2 * k:2 * k + 2]:
            n = C * len(run)
            copy(T.yw[:, W * y + C * run[0]:W * y + C * run[0] + n], p[:, c:c + n]).then_inc(sem["k" + who], 1)
            c += n

    def pick(queue, copy, who, lo=0, hi=S):
        q, off, y = prod[who]
        queue.wait_ge(sem["k" + who], len(runs))
        copy(T.yt[:, S * y + lo:S * y + hi],
             T.yw[:, W * y:W * y + W].indirect(off[:, lo // 16:hi // 16])).then_inc(sem["y" + who], 1)

    def store(queue, who, s, picks=1):
        y = prod[who][2]
        queue.wait_ge(sem["y" + who], picks)
        queue.dma_start(T.y[:, S * y:S * y + S], T.yt[:, S * y:S * y + S]).then_inc(s, 16)

    def acopy(out, in_):
        return a.activation(out, in_, COPY)

    for k, n in enumerate((XC // 4, XC // 2)):
        a.wait_ge(sem.cn, k + 1)
        a.activation(T.cn[:, n:2 * n], T.cn[:, 0:n], ActivationFunctionType.Identity, bias=float(4 * n)).then_inc(sem.cn, 1)
    a.wait_ge(sem.cn, 3)
    a.wait_ge(sem.co, 1)
    acopy(T.val[:], T.cn[:].indirect(T.ov[:])).then_inc(sem.val, 1)
    a.wait_ge(sem.xl, 16)
    a.wait_ge(sem.cw, 4)
    for t in range(4):
        acopy(*sides(own_cols, t)).then_inc(sem.a1, 1)
    for k, grp in enumerate(groups):
        a.wait_ge(sem["l%d" % (k + 1)], lists_in[k])
        for t in range(by_vector[k], 4):
            acopy(*sides(grp, t)).then_inc(sem["a%d" % (k + 1)], 1)
    for k, (first, n, o) in enumerate(PIECES):
        a.wait_ge(sem["t%d" % k], 2)
        for b in range(4):
            c = W * b + C * first
            a.activation(T.xs[:, c:c + C * n], T.xt[:, b:4 * XC].indirect(T.to[:, o:o + 3 * n]), COPY,
                         scale=0.5).then_inc(sem["x%d%d" % (k, b)], 1)
    a.wait_ge(sem.pa0, 1)
    to_slots(acopy, "a", 0)
    a.wait_ge(sem.cs, 1)
    pick(a, acopy, "o")
    for k in (1, 2):
        a.wait_ge(sem["pa%d" % k], 1)
        to_slots(acopy, "a", k)
    a.wait_ge(sem.ls, no + ni)
    pick(a, acopy, "a", 0, S // 2)
    store(a, "a", sem.st2, 2)
    a.wait_ge(sem.st2, 16)

    sy.wait_ge(sem.inv, 1)
    sy.dma_start(T.tb[:], T.cn[0:8, :]).then_inc(sem.tb, 16)
    store(sy, "o", sem.st1)
    store(sy, "i", sem.st1)
    sy.wait_ge(sem.st1, 32)

    def quantise_constants(bb):
        for b in bb:
            v.quantize_mx(T.eq[:, 128 * b:128 * b + 128], T.es[:, 128 * b:128 * b + 128],
                          T.e2[:, 3 - b:3 - b + 512]).then_inc(sem["eq%d" % b], 1)

    v.memset(T.e1[:], 0.5).then_inc(sem.e1, 1)
    v.memset(T.e2[:], 0.0).then_inc(sem.e1, 1)
    for z in (T.ov[:], T.h3[:, 8 * C:4 * Q], T.m0[:, 0:4 * PAD]):
        v.memset(z, 0).then_inc(sem.z, 1)
    v.wait_ge(sem.ip, 1)
    v.tensor_copy(T.po[:], T.pi[:]).then_inc(sem.z, 1)
    v.wait_ge(sem.z, 4)
    v.wait_ge(sem.want, 32)
    for k in range(4):
        v.tensor_scalar(T.wo[32 * k:32 * k + 32, odd:odd + 24], T.wl[0:32, :], 4.0, None, MUL).then_inc(sem.cw, 1)
    v.wait_ge(sem.own, 16)
    v.tensor_copy(T.ov[0:16, :], T.ol[0:16, :]).then_inc(sem.co, 1)
    v.wait_ge(sem.slot, 16)
    v.tensor_scalar(T.s1[0:16, :], T.sl[0:16, :], float(16 * ROW + 1), None, MUL).then_inc(sem.r1, 1)
    v.wait_ge(sem.r1, 1)
    v.tensor_scalar(T.s2[0:16, :], T.s1[0:16, :], 4, 16 * ROW - 1, AluOpType.logical_shift_right,
                    AluOpType.bitwise_and).then_inc(sem.r2, 1)
    v.wait_ge(sem.r2, 1)
    v.tensor_copy(T.po[0:16, :], T.s2[0:16, :]).then_inc(sem.po, 1)
    v.wait_ge(sem.e2, 1)
    quantise_constants([0])
    v.wait_ge(sem.po, 1)
    v.wait_ge(sem.val, 1)
    v.tensor_copy(T.cn[:].indirect(T.po[:]), T.val[:]).then_inc(sem.inv, 1)
    v.wait_ge(sem.xl, 16)
    outs = [(T.c1[:, 0:3 * C], T.c1s[:, 0:3 * C]), (T.oq[:, W:W + 3 * C], T.os_[:, W:W + 3 * C]), (T.iq[:, 0:Q], T.is_[:, 0:Q])]
    for k, grp in enumerate(groups):
        v.wait_ge(sem["l%d" % (k + 1)], lists_in[k])
        for t in range(by_vector[k]):
            v.tensor_copy(*sides(grp, t)).then_inc(sem["v%d" % (k + 1)], 1)
        if k == 2:
            v.wait_ge(sem.slot7, 112)
            v.tensor_copy(T.so[:], T.sl[:]).then_inc(sem.cs, 1)
        v.wait_ge(sem["v%d" % (k + 1)], by_vector[k])
        v.wait_ge(sem["a%d" % (k + 1)], 4 - by_vector[k] + (4 if k == 0 else 0))
        v.quantize_mx(outs[k][0], outs[k][1], grp[0][:]).then_inc(sem["q%d" % (k + 1)], 1)
    v.wait_ge(sem.tb, 16)
    for k, (first, n, o) in enumerate(PIECES):
        for run in runs[2 * k:2 * k + 2]:
            v.tensor_copy(T.to[:, o:o + 3 * len(run)], T.tb[:, 3 * run[0]:3 * (run[-1] + 1)]).then_inc(sem["t%d" % k], 1)
            o += 3 * len(run)
        if k == 0:
            quantise_constants([1, 2, 3])
    banks = [T.pf, T.pn, T.pf]
    for k, (first, n, o) in enumerate(PIECES):
        m, pad = T["m%d" % k], PAD if k == 0 else 0
        for b in range(4):
            v.wait_ge(sem["d%d%d" % (k, b)], 1)
            v.wait_ge(sem["x%d%d" % (k, b)], 1)
            c = W * b + C * first
            v.tensor_tensor(m[:, 4 * pad + b:4 * (pad + C * n):4], banks[k][:, 512 * b:512 * b + C * n],
                            T.xs[:, c:c + C * n], ADD).then_inc(sem["ad%d" % k], 1)
        v.wait_ge(sem["ad%d" % k], 4)
        c = PAD + C * first
        v.quantize_mx(T.mq[:, c - pad:c + C * n], T.ms[:, c - pad:c + C * n], m[:]).then_inc(sem["m%d" % k], 1)
        if k == 0:
            v.wait_ge(sem.wl, 16)
            v.quantize_mx(T.wq[:], T.ws[:], T.wt[:]).then_inc(sem.wq, 1)
    for k in range(3):
        v.wait_ge(sem["po%d" % (k // 2 * 2)], 1)
        to_slots(v.tensor_copy, "o", k)
    for k in range(3):
        v.wait_ge(sem["pi%d" % k], 1)
        to_slots(v.tensor_copy, "i", k)
    v.wait_ge(sem.ls, no + ni)
    pick(v, v.tensor_copy, "i")
    pick(v, v.tensor_copy, "a", S // 2, S)

    def mm(out, l, ls, x, c, n, s):
        pe.matmul_mx(out, l, ls, x[0][:, c:c + n], x[1][:, c + x[2]:c + x[2] + n], True, True).then_inc(s, 1)

    def decode(k, x, c, n):
        for b in range(4):
            pe.wait_ge(sem["eq%d" % b], 1)
            mm(banks[k][:, 512 * b:512 * b + n], T.eq[:, 128 * b:128 * b + 128], T.es[:, 128 * b:128 * b + 128],
               x, c, n, sem["d%d%d" % (k, b)])

    pe.wait_ge(sem.q1, 1)
    pe.wait_ge(sem.ca, 2 * no)
    decode(0, c1, 2 * C, Q)
    pe.wait_ge(sem.cb, 2 * ni + 2 * no)
    decode(1, c2, 0, 3 * C)
    pe.wait_ge(sem.cl, ni + 2 * no)
    pe.wait_ge(sem.ad0, 4)
    decode(2, c3, 0, 3 * C)
    for s in ("wq", "q2", "q3", "m0", "m1"):
        pe.wait_ge(sem[s], 1)
    mm(T.pn[:, 1024:1024 + early], T.wq[:], T.ws[:], mq, PAD, early, sem.po0)
    for k, (first, n, o) in enumerate(PIECES):
        pad = max(0, Q - C * n)
        for who, x, c, count in (("i", iq, Q + C * first - pad, 2 * ni), ("a", oq, W - C * (first + n), 2 * no)):
            p, b, c0 = bank[who][k]
            pe.wait_ge(sem["m%s%d" % (who, k)], count)
            mm(p[:, b:b + C * n + pad], T.wq[:], T.ws[:], x, c, C * n + pad, sem["p%s%d" % (who, k)])
        if k == 0:
            pe.wait_ge(sem.m2, 1)
            mm(T.pf[:, 1536:1536 + W - early], T.wq[:], T.ws[:], mq, PAD + early, W - early, sem.po2)
